import numpy as np, ml_dtypes
CORES = [36,164,52,180,100,228,116,244]
N = 8
BF = ml_dtypes.bfloat16
def gentries(a):
    return np.ascontiguousarray(a.reshape(8, 16, -1).transpose(0, 2, 1)).reshape(8, -1)
def gtable(e):
    e = np.asarray(e); return np.ascontiguousarray(e.reshape(8, -1, 16).transpose(0, 2, 1)).reshape(128, -1).astype(np.int32)
V, W, G, CAP, ST, L, M, RO = 1280, 1728, 64, 16, 5, 256, 3, 4
TOP = 61440 + W - 1
def pick(rng, shape):
    a = rng.integers(0, W, shape); b = ST * rng.integers(0, L, shape) + rng.integers(0, M, shape)
    return np.where(rng.random(shape) < 0.5, b, a)
def parts(rng):
    x = (rng.integers(1, 257, (N, 8, 1, W)) * rng.random((N, 8, 16, W))).astype(np.int64)
    w = np.minimum(rng.integers(0, 16, (N, 8, 16, V)), rng.integers(3, 16, (N, 8, 1, V)))
    k = 4096 * w + pick(rng, (N, 8, 16, V))
    f = (rng.random((N, 8, V)) < rng.choice(np.array([0.3, 0.5, 0.7]), (N, 8, 1))).astype(np.int64)
    t = np.where(rng.random((N, 8, M * L)) < 0.6, rng.integers(0, 2601, (N, 8, M * L)), rng.integers(0, 601, (N, 8, M * L)))
    s = np.ascontiguousarray(np.argsort(rng.random((N, 8, N - 1, L)), axis=-1)[..., :G])
    return x, k, f, t, s
def pack(x, k, f, t, s):
    return {"x0": np.ascontiguousarray(x.reshape(N, 128, W)).astype(np.float32).astype(BF), "kt": np.ascontiguousarray(k.reshape(N, 128, V)).astype(np.int32),
            "f0": np.ascontiguousarray(f).astype(np.int32), "th": np.ascontiguousarray(t).astype(np.int32), "shw": np.stack([gtable(a.reshape(8, -1)) for a in s])}
def setup_inputs(rng):
    return pack(*parts(rng))
def setup_inputs_spread(rng):
    x, k, f, t, s = parts(rng)
    x = np.minimum(np.exp2(8.2 * rng.random((N, 8, 1, W)) * rng.random((N, 8, 16, W))).astype(np.int64) - 1, 255)
    w = np.minimum((16 * rng.random((N, 8, 16, V)) ** rng.choice(np.array([0.3, 1.0, 3.0]), (N, 8, 1, V))).astype(np.int64), 15)
    o = np.argsort(rng.random((N, 8, W)), axis=-1); j = np.minimum((W * rng.random((N, 8, 16 * V)) ** 3).astype(np.int64), W - 1)
    k = 4096 * w + np.take_along_axis(o, j, 2).reshape(N, 8, 16, V)
    f = (rng.random((N, 8, V)) < rng.choice(np.array([0.05, 0.5, 0.95]), (N, 8, 1))).astype(np.int64)
    t = np.minimum(np.exp2(12 * rng.random((N, 8, M * L))).astype(np.int64) - 1, 4080)
    s = np.minimum((L * rng.random((N, 8, N - 1, G)) ** 2).astype(np.int64), L - 1)
    return pack(x, k, f, t, s)
def setup_inputs_ends(rng):
    last = ST * (L - 1) + M - 1
    x = 255 * rng.integers(0, 2, (N, 8, 16, W)); kind = rng.integers(0, 3, (N, 8, 1, W))
    x = np.where(kind == 0, 0, np.where(kind == 1, 255, x))
    x[..., W - 1] = 255; x[:, 3, :, W - 1] = 255 * rng.integers(0, 2, (N, 16)); x[:, 5, :, W - 1] = 0
    k = TOP * rng.integers(0, 2, (N, 8, 16, V)); kind = rng.integers(0, 10, (N, 8, 1, V))
    e = 61440 * rng.integers(0, 2, (N, 8, 16, V)) + rng.choice(np.array([0, 1, V - 1, last, V, W - 1]), (N, 8, 16, V))
    k = np.where(kind < 2, 0, np.where(kind < 4, TOP, np.where(kind < 7, k, e)))
    for m in range(M):
        for i in (1, 2, L - 1):
            x[..., ST * i + m] = 0; k[..., ST * i + m] = TOP
        x[..., ST * (L - 2) + m] = 0; k[..., ST * (L - 2) + m] = 0
        x[..., ST * 3 + m] = 255; k[..., ST * 3 + m] = 0
    k[..., V - 1] = TOP
    f = rng.integers(0, 2, (N, 8, V)); f[:, ::2, V - 1] = 1
    t = 4080 * rng.integers(0, 2, (N, 8, M * L))
    z = ST * np.arange(L); xv = x[..., z]; flat = np.all(xv == xv[:, :, :1], axis=2)
    f[..., z] = np.where(flat, 1, f[..., z]); t[..., :L] = 4080 * (1 - f[..., z])
    f[1::2, 7, ST * (L - 1)] = 0; t[1::2, 7, L - 1] = 4080
    for m in range(1, M):
        t[..., m * L + 2] = 4080; t[..., m * L + L - 1] = 4080
    s = np.where(rng.random((N, 8, N - 1, G)) < 0.75, (L - 1) * rng.integers(0, 2, (N, 8, N - 1, G)), rng.integers(0, L, (N, 8, N - 1, G)))
    return pack(x, k, f, t, s)
def setup_inputs_corners(rng):
    x, k, f, t, s = parts(rng); own = np.arange(V); h = L // 2
    k = 4096 * rng.choice(np.array([0, 15, 15]), (N, 8, 16, V)) + (k & 4095)
    f[:, 2] = 0; f[:, 4] = 1; f[:, 6] = 1
    k[:, 1] = (k[:, 1] & 61440) + own; k[:, 3] = k[:, 3] & 61440
    k[:, 5] = (k[:, 5] & 61440) + rng.choice(np.array([V - 1, W - 1]), (N, 16, V)); k[:, 6] = 61440 + np.maximum(own - 1, 0)
    t = np.where(rng.random(t.shape) < 0.3, 4080 * rng.integers(0, 2, t.shape), t)
    x[..., W - 1] = rng.integers(2, 256, (N, 8, 16))
    for q in range(N):
        for g in range(8):
            o = rng.permutation(L); a, b = o[:h], o[h:]; xx = x[q, g]; kk = k[q, g]
            xx[:, ST * a] = 0; kk[rng.integers(0, 16, h), ST * a] = TOP
            kk[:, ST * b] = 61440 + ST * b
            b2 = b[:h // 4]; u = rng.integers(0, 2, (16, h // 4)); u[0] = 1
            xx[:, ST * b2] = xx[:, W - 1:W] - u; kk[:, ST * b2] = TOP; t[q, g, b2] = 0
            for d in range(N - 1):
                n = int(rng.choice(np.array([0, 1, CAP - 1, CAP, CAP + 1, G])))
                if (q == 0 and d == 0) or (q == N - 1 and d == N - 2): n = (CAP, CAP + 1, G, CAP - 1, 1, 0, CAP + 1, CAP)[g]
                s[q, g, d] = rng.permutation(np.concatenate([a[rng.integers(0, h, n)], b[rng.integers(0, h, G - n)]]))
    return pack(x, k, f, t, s)
def setup_inputs_crowd(rng):
    x, k, f, t, s = parts(rng); z = ST * np.arange(L); h2 = L // 2
    for q in range(N):
        for g in range(8):
            xx = x[q, g]; kk = k[q, g]
            if g % 2 == 1:
                hub = int(ST * rng.integers(0, L) + M - 1); was = np.array(kk); j = int(rng.integers(0, V)); one = int(rng.integers(0, L))
                kk[:] = (kk & 61440) + hub; kk[:, hub] = was[:, hub]; s[q, g] = one
                if g < 4: f[q, g, hub] = 1
                if g % 4 == 3:
                    kk[:, j] = was[:, j]; s[q, g, :, G - 1] = (one + 1) % L
            flip = np.ones(L, bool)
            if q % 4 == 1 and g == 7: flip[L - 1] = False
            if q % 4 == 2 and g % 2 == 1: flip[int(rng.integers(0, L))] = False
            if q % 4 == 3:
                flip[:] = g == 0
                flip[int(rng.integers(0, L))] = False
            xx[0, z] = rng.integers(1, 255, L)
            t[q, g, :L] = np.where(flip == (f[q, g, z] == 1), 0, 4080)
            xx[:, V - 1] = 255; f[q, g, V - 1] = 0
            i = rng.permutation(L)[:h2]; u = rng.integers(4, 255, (16, h2))
            xx[:, ST * i + 1] = 255 - u; kk[:, ST * i + 1] = 61440 + V - 1
            t[q, g, L + i] = np.add.reduce(u, axis=0) - rng.integers(0, 64, h2)
    return pack(x, k, f, t, s)
def setup_inputs_ties(rng):
    x, k, f, t, s = parts(rng); h = L // 2
    rec = 4096 * rng.integers(0, 16, (N, 8, 16, 1)) + pick(rng, (N, 8, 16, 1))
    lane = (np.arange(V) % ST) < M
    e = np.where(lane & (rng.random((N, 8, 16, V)) < 0.5), 61440 + pick(rng, (N, 8, 16, V)), rec)
    k[:, 1::2] = e[:, 1::2]; k[:, 2, 8:] = k[:, 2, :8]; k[:, 4, 1:] = np.where(rng.random((N, 15, V)) < 0.5, k[:, 4, :1], k[:, 4, 1:])
    x[..., V - 1] = 255; f[..., V - 1] = 0
    for q in range(N):
        for g in range(8):
            i = rng.permutation(L)[:h]; u = rng.integers(4, 255, (16, h)); xx = x[q, g]; kk = k[q, g]
            xx[:, ST * i] = 255 - u; kk[:, ST * i] = 61440 + V - 1
            t[q, g, i] = np.add.reduce(u, axis=0) + rng.integers(-1, 2, h)
    return pack(x, k, f, t, s)
def check_inputs(d):
    bad = []
    for a, lo, hi in (("x0", 0, 255), ("kt", 0, TOP), ("f0", 0, 1), ("th", 0, 4080), ("shw", 0, L - 1)):
        v = np.asarray(d[a]).astype(np.float64)
        if not (np.min(v) >= lo and np.max(v) <= hi): bad.append("range of " + a)
    v = np.asarray(d["x0"]).astype(np.float64)
    if not np.all(v == np.floor(v)): bad.append("whole numbers of x0")
    if np.max(np.asarray(d["kt"]).astype(np.int64) & 4095) >= W: bad.append("masters of kt")
    return bad
def reference(x0, kt, f0, th, shw):
    x = x0.astype(np.float32).astype(np.int64).reshape(N, 8, 16, W)
    k0 = kt.astype(np.int64).reshape(N, 8, 16, V); k = np.array(k0)
    f = np.zeros((N, 8, W), np.int64); f[..., :V] = f0
    o = np.zeros((N, 8, 16, V), np.int64) + np.arange(V)
    lim = th.astype(np.int64).reshape(N, 8, M, L)
    s = np.stack([gentries(a) for a in shw]).astype(np.int64).reshape(N, 8, N - 1, G)
    num = np.zeros(N, np.int64)
    for rnd in range(RO):
        m = rnd % M; v = ST * np.arange(L) + m
        ov = o[..., v]; fo = np.take_along_axis(f, ov.reshape(N, 8, 16 * L), 2).reshape(N, 8, 16, L)
        back = (ov != v) & (fo == 0)
        kv = np.where(back, k0[..., v], k[..., v]); ov = np.where(back, v, ov); k[..., v] = kv
        c = kv & 4095; w = kv >> 12
        fc = np.take_along_axis(f, c.reshape(N, 8, 16 * L), 2).reshape(N, 8, 16, L)
        best = np.where(fc == 0, kv, -1)
        for j in range(16):
            e = np.take_along_axis(k, np.minimum(c[:, :, j], V - 1)[:, :, None, :], 3)
            cand = 4096 * np.minimum(w[:, :, j][:, :, None, :], e >> 12) + (e & 4095)
            win = (fc[:, :, j] == 1)[:, :, None, :] & (cand > best)
            best = np.where(win, cand, best); ov = np.where(win, c[:, :, j][:, :, None, :], ov)
        k[..., v] = best; o[..., v] = ov
        c = best & 4095; w = best >> 12; y = np.zeros((N, 8, 16, L), np.int64)
        for j in range(16):
            e = np.take_along_axis(x, c[:, :, j][:, :, None, :], 3)
            y = np.maximum(y, np.minimum(e, 17 * w[:, :, j][:, :, None, :]))
        xv = x[..., v]; dist = np.add.reduce(np.abs(xv - y), axis=2)
        st = (dist < lim[:, :, m] + (num & 63)[:, None, None]).astype(np.int64)
        nx = np.where((st == 1)[:, :, None, :], y, (xv + y) >> 1)
        num = np.add.reduce((st != f[..., v]).astype(np.int64).reshape(N, 8 * L), axis=1)
        f[..., v] = st; x[..., v] = nx
        ch = np.any(nx != xv, axis=2).astype(np.int64)
        for a in range(N):
            for d in range(N - 1):
                q = (a + 1 + d) % N; ix = s[q, :, d]; h = np.take_along_axis(ch[q], ix, 1)
                go = (h == 1) & (np.add.accumulate(h, axis=1) - h < CAP); lo = V + d * G
                x[a, :, :, lo:lo + G] = np.where(go[:, None, :], np.take_along_axis(nx[q], ix[:, None, :], 2), x[a, :, :, lo:lo + G])
    yk = np.add.reduce(k.reshape(N, 128, L, ST)[..., :M], axis=3); yo = np.add.reduce(o.reshape(N, 128, L, ST)[..., :M], axis=3)
    return {"yx": x.reshape(N, 128, W).astype(np.float32).astype(BF), "yf": f[..., :V].astype(np.float32), "yk": yk.astype(np.float32), "yo": yo.astype(np.float32)}

@@ -1,0 +1,766 @@
+import numpy as np
+from concourse.bass import DstId, RemoteDMATransfer
+from concourse.mybir import AluOpType as OP, ActivationFunctionType as AF
+
+N, V, W, G, L, RO = 8, 1280, 1728, 64, 256, 4
+NS = (N - 1) * G
+SW = 131072.0
+CW = 1.5 * 2.0 ** 40
+C1 = 1.5 * 2.0 ** 23
+OOWN = 90112.0
+OACC = 57856.0
+PAD = 16
+
+B, F, I, U = "bfloat16", "float32", "int32", "uint16"
+_SB = dict(
+    ktb=(V, I), shb=(28, I), sho=(28, U), X=(W, B), O32=(V, F), Wall=(V, B), Wt=(W, B), Mt=(W, F),
+    Gw=(4096, B), A=(4096 + PAD, B), Gm=(4096, F), S=(4096, F), Gx=(4096, B), A3=(4096, B), S3=(4096, B),
+    ones=(512, B), Id=(128, B), NI=(128, B), H=(128, B), N256=(128, B), I32=(128, B), N512=(128, B), P125=(128, B),
+    Blk=(128, B), Blk0=(128, B), Sel=(2048, B), Dg=(2048, B), Dz=(17 * 128, B),
+    If=(128, F), If32=(128, F), NIf512=(128, F), on16=(128, F),
+    cst=(512, B), c16=(NS, B), cmh=(L, B), mask3=(2048, B), mask5=(NS, B), vt=(V, F),
+    pk=(16, I), pk2=(16, I), ek=(16, F), ek32=(16, F), kq=(1, F), kq2=(1, F), colh=(1, F),
+    offC=(RO * L, U), offX=(L, U), offO=(L, U), h128=(L, B), hi=(RO * L, B), lo=(RO * L, B),
+    b1=(L, F), Bi=(L, I), Mi=(L, I), lowi=(L, I), z=(RO * L, B), Wn=(RO * L, B), w17=(L, B),
+    fs=(80, I), fsb=(80, B), ths=(48, I), thf=(48, F), fo=(L, B), st=(L, B), ad=(L, B), ad2=(L, B), NI32=(128, B), NIf32=(128, F), u=(L, B), nx=(L, B), ne=(L, B), chb=(L, B), junk=(L, B),
+    Gs=(NS, B), Gh=(NS, B), cum=(NS, B), outb=(RO * NS, B), land=(RO * NS, B), rl=(NS, B),
+    acc=(512, F), Oacc=(RO * L, F), sq=(RO * L, F), cnt=(2, F), Ai=(1, I), Ai2=(1, I), acol=(1, F),
+    O0p=(L, F), dO=(L, F), ne0=(L, B), ne32=(L, B), dM=(L, F), dW=(L, B), dWf=(L, B),
+    wb3=(L, B), Op3=(L, F), yfb=(V, F), ykb=(L, F), yob=(L, F),
+)
+_S8 = dict(f8b=(V, B), th8f=(768, F), E8=(128, B), NE8=(128, F), NE8b=(128, B))
+SCRATCH = {}
+for _n, (_w, _d) in _SB.items():
+    SCRATCH[_n] = ("sbuf", [128, _w], _d)
+for _n, (_w, _d) in _S8.items():
+    SCRATCH[_n] = ("sbuf", [8, _w], _d)
+for _k in range(8):
+    SCRATCH["ps%d" % _k] = ("psum", [128, 512], F)
+
+LOADS = ["l_f", "l_k0", "l_k1", "l_k2", "l_th", "l_sh", "l_x", "l_f8", "l_t8"]
+SEMAPHORES = ["e_v", "e_a", "e_t", "e_g", "stored", "sent"] + LOADS + ["arr%d" % t for t in range(RO)]
+
+MODELS = [(1.04, 1.56, 0.55, 30.0, 140.0, 1.0), (1.04, 1.15, 0.5, 20.0, 80.0, 0.5), (1.04, 1.95, 0.6, 40.0, 200.0, 0.5)]
+SEED = 1
+MOVES = 6000
+HEAT = 600.0
+PASSES = 8
+GCH = 1024
+WACT = (320, 960)
+FUSED = ((0, 0), (3, 0))
+GMV = ()
+GWV = ()
+GXV = ()
+CH = ((0, 64), (64, 128), (192, 64))
+TURNS = "A0 A0 A1 S0 A1 S0 A1 A1 S1 A2 S1 A2 S1 S1 S2 S2 X0 X0 X1 X1 X1 X1 X2 X2"
+NFIL = 2
+CONST = ("Id", "NI", "H", "N256", "I32", "N512", "P125", "Blk", "Sel", "Dg", "Dz", "If", "If32", "NIf512", "on16", "cst", "c16",
+         "cmh", "E8", "NE8", "NE8b", "NI32", "NIf32")
+ZPE = True
+
+
+def R(name, a=0, b=None, s=1):
+    if b is None:
+        b = SCRATCH[name][1][1]
+    return (name, a, b, s)
+
+
+def cnt_of(r):
+    return len(range(r[1], r[2], r[3]))
+
+
+def two(r):
+    return SCRATCH[r[0]][2] in (B, U)
+
+
+def isps(r):
+    return SCRATCH[r[0]][0] == "psum"
+
+
+def build():
+    ops = []
+    unit = [None]
+
+    def add(e, kind, args, reads, writes, cost):
+        ops.append(dict(e=e, kind=kind, a=args, r=[x for x in reads if isinstance(x, tuple)], w=writes,
+                        c=cost if isinstance(cost, tuple) else ("k", cost), u=unit[0]))
+
+    def vc(n, rate):
+        return ("v", n * rate)
+
+    def ts(out, in0, s1, op0, s2=None, op1=None):
+        add("v", "ts", (out, in0, s1, s2, op0, op1), [in0, s1, s2], [out], vc(cnt_of(out), 0.5 if two(out) and two(in0) else 1))
+
+    def tt(out, a, b, op):
+        add("v", "tt", (out, a, b, op), [a, b], [out], vc(cnt_of(out), 1 if isps(a) or isps(b) else 2))
+
+    def cp(out, a):
+        add("v", "cp", (out, a), [a], [out], vc(cnt_of(out), 0.5 if two(out) and two(a) else 1))
+
+    def ms(out, val):
+        add("v", "ms", (out, val), [], [out], vc(cnt_of(out), 0.5 if two(out) else 1))
+
+    def scan(out, d0, d1, op0, op1):
+        add("v", "scan", (out, d0, d1, op0, op1), [d0, d1], [out], vc(cnt_of(out), 0.5 if two(out) and two(d0) and two(d1) else 1))
+
+    def act(out, a, func, bias=0.0, scale=1.0, accum=None):
+        add("a", "act", (out, a, func, bias, scale, accum), [a, bias, scale], [out] + ([accum] if accum else []), vc(cnt_of(out), 1))
+
+    def gather(e, out, win, off, plus=None):
+        n = cnt_of(out)
+        parts = max(1, n // GCH)
+        for j in range(parts):
+            o = (out[0], out[1] + j * n // parts, out[1] + (j + 1) * n // parts, 1)
+            f = (off[0], off[1] + j * n // parts // 16, off[1] + (j + 1) * n // parts // 16, 1)
+            p = None if plus is None else (plus[0], plus[1] + j * n // parts, plus[1] + (j + 1) * n // parts, 1)
+            add(e, "gat", (o, win, f, p), [win, f, p], [o], ("g", n / parts))
+
+    def mm(out, terms):
+        alone = unit[0] is None
+        for j, (l, r) in enumerate(terms):
+            if alone and (j % 6 == 0 or not two(l)):
+                unit[0] = len(ops)
+            add("t", "mm", (out, l, r, j == 0, j == len(terms) - 1), [l, r], [out],
+                ("p", max(64, cnt_of(out)) * (1 if two(l) else 4)))
+        if alone:
+            unit[0] = None
+
+    def mat(name, k=0):
+        return R(name, 128 * k, 128 * k + 128)
+
+    def P(bank, a, n):
+        return R("ps%d" % bank, a, a + n)
+
+    rot = [0]
+
+    def big():
+        rot[0] += 1
+        return NFIL + (rot[0] - 1) % (6 - NFIL)
+
+    rot2 = [0]
+
+    def fil():
+        rot2[0] += 1
+        return (rot2[0] - 1) % NFIL
+
+    add("s", "load", ("l_k0", "ktb", "kt", 0, 320), [], [R("ktb", 0, 320)], 2600)
+    add("a", "load", ("l_k1", "ktb", "kt", 320, 640), [], [R("ktb", 320, 640)], 3000)
+    add("s", "load", ("l_k2", "ktb", "kt", 640, V), [], [R("ktb", 640, V)], 3600)
+    add("a", "load", ("l_f", "fs", "f0", None, None), [], [R("fs")], 3000)
+    add("s", "load", ("l_th", "ths", "th", None, None), [], [R("ths")], 3600)
+    add("s", "load", ("l_sh", "shb", "shw", 0, 28), [], [R("shb")], 2200)
+    add("s", "load", ("l_x", "X", "x0", 0, W), [], [R("X")], 4000)
+    ms(R("ones"), 1.0)
+    add("g", "iota", (R("pk"), [[-1, 16]], 16, 1), [], [R("pk")], 200)
+    add("g", "sel", (R("Id"), mat("ones"), [[-1, 128]], OP.is_equal, 0, 1, 0.0), [R("ones")], [R("Id")], 430)
+    add("g", "sel", (R("Blk0"), mat("ones"), [[-16, 8], [0, 16]], OP.is_ge, 0, 1, 0.0), [R("ones")], [R("Blk0")], 430)
+    add("g", "sel", (R("Blk"), R("Blk0"), [[16, 8], [0, 16]], OP.is_ge, 15, -1, 0.0), [R("Blk0")], [R("Blk")], 430)
+    add("g", "sel8", (R("E8"), R("ones"), [[1, 8], [0, 16]], OP.is_equal, 0, -1), [R("ones")], [R("E8")], 430)
+    add("g", "iota", (R("vt"), [[1, V]], int(-OOWN), 0), [], [R("vt")], 2700)
+    ts(R("pk2"), R("pk"), 15, OP.bitwise_and)
+    ts(R("ek"), R("pk2"), 0.0, OP.is_equal)
+    ts(R("ek32"), R("ek"), -32.0, OP.mult)
+    ts(R("kq"), R("pk2", 0, 1), -7.5, OP.add)
+    tt(R("kq2"), R("kq"), R("kq"), OP.mult)
+    ts(R("colh"), R("kq2"), -2048.0, OP.mult, 512.0 + 57344.0 - 32768.0, OP.add)
+    for nm, val in (("NI", -1.0), ("H", 0.5), ("N256", -256.0), ("I32", 1 / 32), ("N512", -512.0), ("P125", 12544.0),
+                    ("If", 1.0), ("If32", 1 / 32), ("NIf512", -512.0), ("NI32", -1 / 32), ("NIf32", -1 / 32)):
+        ts(R(nm), R("Id"), val, OP.mult)
+    ts(R("NE8"), R("E8"), -1.0, OP.mult)
+    ts(R("NE8b"), R("E8"), -1.0, OP.mult)
+    for k in range(16):
+        act(mat("Sel", k), R("Blk"), AF.Identity, scale=R("ek", k, k + 1))
+        if k % 2:
+            ts(mat("Dg", k), R("Id"), R("ek32", k, k + 1), OP.mult)
+        else:
+            act(mat("Dg", k), R("Id"), AF.Identity, scale=R("ek32", k, k + 1))
+    for k in range(17):
+        ts(mat("Dz", k), R("Id"), 1024.0 * (2 * (k - 1) - 15), OP.mult)
+    ms(R("on16"), 1 / 16)
+    ms(R("c16"), 16.0)
+    ms(R("cmh"), -0.5)
+    add("g", "sel", (R("cst"), R("ones"), [[0, 32], [1, 16]], OP.is_gt, 0, 0, -2.0 ** 22), [R("ones")], [R("cst")], 1300)
+    add("g", "iota", (R("mask3"), [[0, 128], [256, 16]], 0, 0), [], [R("mask3")], 4500)
+    add("g", "iota", (R("mask5"), [[0, N - 1], [G, G]], 0, 0), [], [R("mask5")], 1100)
+    ms(R("A", 0, PAD), 0.0)
+    ms(R("Wt", V, W), 0.0)
+    ms(R("Mt", V, W), 0.0)
+    ms(R("cnt"), 0.0)
+    cp(R("fsb"), R("fs"))
+    cp(R("thf"), R("ths"))
+    add("s", "load", ("l_f8", "f8b", "fsb", None, None), [R("fsb")], [R("f8b")], 2200)
+    add("s", "load", ("l_t8", "th8f", "thf", None, None), [R("thf")], [R("th8f")], 2200)
+    cp(R("sho"), R("shb"))
+    for a, b in ((0, 320), (320, 640), (640, 960), (960, V)):
+        ts(R("O32", a, b), R("ktb", a, b), 32.0, OP.mult, SW, OP.add)
+        if a in WACT:
+            act(R("Gw", a, b), R("O32", a, b), AF.Identity, bias=128.0, scale=1 / SW)
+            act(R("Wall", a, b), R("Gw", a, b), AF.Identity, bias=-128.0 * SW, scale=SW)
+        else:
+            ts(R("Wall", a, b), R("O32", a, b), CW, OP.add, CW, OP.subtract)
+        bk = big()
+        mm(P(bk, 0, b - a), [(R("If"), R("O32", a, b)), (R("NI"), R("Wall", a, b))])
+        act(R("Mt", a, b), P(bk, 0, b - a), AF.Identity)
+        bk = fil()
+        for q in range(4):
+            mm(P(bk, 80 * q, 80), [(mat("Sel", a // 80 + q), R("fsb"))])
+        tt(R("Wt", a, b), R("Wall", a, b), P(bk, 0, b - a), OP.mult)
+
+    def lanes(name, m, h=None):
+        if h is None:
+            return R(name, m, V, 5)
+        return R(name, m + 5 * CH[h][0], 5 * (CH[h][0] + CH[h][1]), 5)
+
+    def tile(name, t, h=None):
+        if h is None:
+            return R(name, t * L, t * L + L)
+        return R(name, t * L + CH[h][0], t * L + CH[h][0] + CH[h][1])
+
+    def wide(name, h, pad=0):
+        return R(name, pad + 16 * CH[h][0], pad + 16 * (CH[h][0] + CH[h][1]))
+
+    def prep_off(t):
+        ts(tile("offC", t), lanes("Mt", t % 3), 1 / 32, OP.mult)
+
+    def prep_pieces(t):
+        m = t % 3
+        act(R("h128"), lanes("Mt", m), AF.Identity, bias=128.0, scale=1 / 8192)
+        act(tile("hi", t), R("h128"), AF.Identity, bias=R("colh"), scale=256.0)
+        bk = fil()
+        mm(P(bk, 0, L), [(R("If32"), lanes("Mt", m)), (R("N256"), R("h128"))])
+        act(tile("lo", t), P(bk, 0, L), AF.Identity, bias=32768.0)
+
+    def gm(t, h):
+        if (t, h) not in FUSED:
+            gather("v" if (t, h) in GMV else "a", wide("Gm", h), R("Mt"), tile("offC", t, h))
+
+    def origin(t, oprev):
+        act(tile("sq", t), tile("z", t), AF.Square)
+        for j in range(8):
+            bk = fil()
+            for q in range(2):
+                k = 2 * j + q
+                mm(P(bk, L * q, L), [(mat("Sel", k), tile("hi", t)), (mat("Sel", k), tile("lo", t)), (mat("Dz", k + 1), tile("z", t))])
+            if j == 0:
+                act(R("acc"), P(bk, 0, 512), AF.Identity)
+            else:
+                tt(R("acc"), R("acc"), P(bk, 0, 512), OP.max)
+        bk = fil()
+        mm(P(bk, 0, L), [(R("If"), oprev), (mat("Dz", 0), tile("z", t))])
+        tt(P(bk, L, L), R("acc", 0, L), P(bk, 0, L), OP.max)
+        tt(tile("Oacc", t), R("acc", L, 512), P(bk, L, L), OP.max)
+
+    def merge(t):
+        ld = R("land", t * NS, t * NS + NS)
+        add("x", "arr", (t,), [R("outb", t * NS, t * NS + NS)], [ld], 9000)
+        act(R("rl"), ld, AF.Relu, bias=1.0)
+        mm(P(7, 0, NS), [(R("Id"), R("X", V, W)), (R("N256"), R("rl"))])
+        tt(R("X", V, W), ld, P(7, 0, NS), OP.max)
+
+    prep_off(0)
+    gm(0, 0)
+    for t in range(RO):
+        m = t % 3
+        if t == 3:
+            b1, b2, b3 = big(), big(), big()
+            for h in range(2):
+                gather("av"[h], R("Gx", 2048 * h, 2048 * h + 2048), R("Wt"), R("offO", 128 * h, 128 * h + 128))
+                mm(P(b1, 128 * h, 128), [(mat("Dg", k), R("Gx", 2048 * h + k, 2048 * h + 2048, 16)) for k in range(16)])
+            fr = P(b2, 0, L)
+            act(fr, P(b1, 0, L), AF.Relu, bias=1.0)
+            tt(P(b1, 0, L), R("dM"), fr, OP.mult)
+            tt(P(b1, L, L), R("dWf"), fr, OP.mult)
+            tt(lanes("Mt", 0), lanes("Mt", 0), P(b1, 0, L), OP.add)
+            tt(lanes("Wt", 0), lanes("Wt", 0), P(b1, L, L), OP.add)
+            prep_off(3)
+            tt(P(b3, 0, L), R("dW"), fr, OP.mult)
+            tt(P(b3, L, L), R("dO"), fr, OP.mult)
+            tt(R("wb3"), tile("Wn", 0), P(b3, 0, L), OP.add)
+            tt(R("Op3"), R("O0p"), P(b3, L, L), OP.add)
+            gm(3, 0)
+        if t in (0, 3):
+            prep_pieces(t)
+        for h in range(len(CH)):
+            gather("v" if (t, h) in GWV else "a", wide("Gw", h), R("Wt"), tile("offC", t, h))
+        for h in range(1, len(CH)):
+            gm(t, h)
+
+        def clamp(out, pad, src, wts, h):
+            o, n = 16 * CH[h][0], CH[h][1]
+            per = min(16, 512 // n)
+            for k0 in range(0, 16, per):
+                bk = big()
+                ks = range(k0, min(16, k0 + per))
+                unit[0] = len(ops)
+                for k in ks:
+                    mm(P(bk, n * (k - k0), n), [(mat("Sel", k), wts)])
+                for k in ks:
+                    tt(R(out, pad + o + k, pad + o + 16 * n, 16), R(src, o + k, o + 16 * n, 16), P(bk, n * (k - k0), n), OP.min)
+                unit[0] = None
+                if k0 + per < 16:
+                    yield
+
+        def step2a(h):
+            yield from clamp("A", PAD, "Gw", lanes("Wall", m, h) if t < 3 else tile("wb3", 0, h), h)
+            yield
+
+        def step2b(h):
+            wb = lanes("Wall", m, h) if t < 3 else tile("wb3", 0, h)
+            o, n = 16 * CH[h][0], CH[h][1]
+            fused = (t, h) in FUSED
+            if fused:
+                gather("v", wide("Gm", h), R("Mt"), tile("offC", t, h), wide("A", h, PAD))
+            for a in range(o, o + 16 * n, 512):
+                if a > o:
+                    yield
+                if fused:
+                    scan(R("S", a, a + 512), R("cst"), R("Gm", a, a + 512), OP.add, OP.max)
+                    continue
+                bk = big()
+                mm(P(bk, 0, 512), [(R("Id"), R("cst")), (R("Id"), R("A", PAD + a - 1, PAD + a + 511)), (R("NI"), R("A", PAD + a, PAD + a + 512))])
+                scan(R("S", a, a + 512), P(bk, 0, 512), R("Gm", a, a + 512), OP.add, OP.max)
+            a15 = R("A", PAD + o + 15, PAD + o + 16 * n, 16)
+            s15 = R("S", o + 15, o + 16 * n, 16)
+            p1, p3 = P(6, o // 8, n), P(6, o // 8 + n, n)
+            own = [(R("If"), lanes("O32", m, h))] if t < 3 else [(R("If"), lanes("Mt", m, h)), (R("Id"), wb)]
+            mm(p1, own + [(R("Id"), R("c16", 0, n))] + [(mat("Dg", k), R("Gw", o + k, o + 16 * n, 16)) for k in range(16)]
+               + ([] if fused else [(R("NI"), a15)]))
+            if fused:
+                tt(tile("Bi", 0, h), s15, p1, OP.max)
+            else:
+                mm(p3, [(R("Id"), a15)])
+                tt(tile("b1", 0, h), s15, p1, OP.max)
+                tt(tile("Bi", 0, h), tile("b1", 0, h), p3, OP.add)
+            ts(tile("Mi", 0, h), tile("Bi", 0, h), 5, OP.logical_shift_right, 4095, OP.bitwise_and)
+            cp(tile("offX", 0, h), tile("Mi", 0, h))
+            ts(tile("Wn", t, h), tile("Bi", 0, h), CW, OP.add, CW, OP.subtract)
+            act(tile("w17", 0, h), tile("Wn", t, h), AF.Identity, bias=-17.0, scale=17 / SW)
+            if h < len(CH) - 1:
+                yield
+                return
+            ts(lanes("Mt", m), R("Mi"), 32.0, OP.mult)
+            if any((t, j) in FUSED for j in range(len(CH))) or not ZPE:
+                ts(R("lowi"), R("Bi"), 31, OP.bitwise_and)
+                ts(tile("z", t), R("lowi"), -2.0, OP.mult, 15.0, OP.add)
+            else:
+                bk = fil()
+                mm(P(bk, 0, L), [(R("If32"), R("b1")), (R("I32"), R("A", PAD + 15, PAD + 4096, 16)),
+                                 (R("NI32"), tile("Wn", t)), (R("NIf32"), lanes("Mt", m))])
+                act(tile("z", t), P(bk, 0, L), AF.Identity, bias=15.0, scale=-64.0)
+            yield
+
+        def step3(h):
+            if h == 0 and t > 0:
+                merge(t - 1)
+            gather("v" if (t, h) in GXV else "a", wide("Gx", h), R("X"), tile("offX", 0, h))
+            yield from clamp("A3", 0, "Gx", tile("w17", 0, h), h)
+            scan(wide("S3", h), R("mask3", 0, 16 * CH[h][1]), wide("A3", h), OP.min, OP.max)
+            yield
+
+        work = {}
+        for w in TURNS.split():
+            if w not in work:
+                work[w] = {"A": step2a, "S": step2b, "X": step3}[w[0]](int(w[1]))
+            next(work[w])
+        assert len(work) == 3 * len(CH) and all(next(w, 1) == 1 for w in work.values())
+        if t < 2:
+            prep_off(t + 1)
+            prep_pieces(t + 1)
+            gm(t + 1, 0)
+        if t == 3:
+            bk = fil()
+            mm(P(bk, 0, L), [(R("I32"), tile("Wn", j)) for j in (1, 2, 3)] + [(R("If32"), lanes("Mt", j)) for j in range(3)])
+            act(R("ykb"), P(bk, 0, L), AF.Identity, bias=-3 * 4096.0)
+            add("s", "store", ("yk", "ykb", 0, L), [R("ykb")], [], 2000)
+            origin(3, R("Op3"))
+        y = R("S3", 15, 4096, 16)
+        x = lanes("X", m)
+        mm(P(6, L, L), [(R("Id"), tile("Wn", t))])
+        mm(P(6, 0, L), [(R("NI"), x), (R("Id"), y)])
+        act(R("ad"), P(6, 0, L), AF.Abs)
+        act(R("ad2"), P(6, 0, L), AF.Abs, bias=-0.5)
+        mm(P(7, 0, L), [(R("NE8"), R("th8f", m * L, m * L + L)), (R("Blk"), R("ad"))])
+        mm(P(7, L, L), [(R("Blk"), R("ad"))])
+        ts(R("st"), P(7, 0, L), 0.0 if t == 0 else R("acol"), OP.is_lt)
+        tt(R("ne"), R("st"), P(7, L, L), OP.mult)
+        tt(lanes("Wt", m), R("st"), P(6, L, L), OP.mult)
+        tt(R("u"), R("st"), P(6, 0, L), OP.mult)
+        mm(P(7, 0, L), [(R("Blk"), R("cmh")), (R("Blk"), R("ad2")), (R("Id"), R("ne"))])
+        act(R("chb"), P(7, 0, L), AF.Sign)
+        mm(P(6, 0, L), [(R("H"), R("cmh")), (R("H"), x), (R("H"), y), (R("H"), R("u"))])
+        ts(R("nx"), P(6, 0, L), C1, OP.add, C1, OP.subtract)
+        gather("a", R("Gh"), R("chb"), R("sho"))
+        gather("v" if t == 3 else "a", R("Gs"), R("nx"), R("sho"))
+        add("g", "pcp", (x, R("nx")), [R("nx")], [x], 750)
+        scan(R("cum"), R("mask5"), R("Gh"), OP.min, OP.add)
+        mm(P(7, 0, NS), [(R("N256"), R("c16")), (R("P125"), R("Gh")), (R("N512"), R("cum"))])
+        ob = R("outb", t * NS, t * NS + NS)
+        tt(ob, R("Gs"), P(7, 0, NS), OP.min)
+        add("g", "send", (t,), [ob], [], 500)
+        if t < 3:
+            mm(P(7, 0, L), [(R("Id"), R("st")), (R("NE8b"), lanes("f8b", m))])
+            act(R("junk"), P(7, 0, L), AF.Abs, accum=R("cnt", 0, 1))
+            mm(P(7, 0, 2), [(R("on16"), R("cnt"))])
+            cp(R("Ai"), P(7, 0, 1))
+            ts(R("Ai2"), R("Ai"), 63, OP.bitwise_and)
+            cp(R("acol"), R("Ai2"))
+            origin(t, lanes("vt", m))
+        if t == 0:
+            bk = fil()
+            mm(P(bk, 0, L), [(R("If"), tile("Oacc", 0)), (R("NIf512"), tile("sq", 0))])
+            act(R("O0p"), P(bk, 0, L), AF.Identity, bias=-(OACC + OOWN))
+            ts(R("offO"), R("O0p"), OOWN, OP.add)
+            tt(R("dO"), lanes("vt", 0), R("O0p"), OP.subtract)
+            ts(R("ne0"), R("dO"), 0.0, OP.not_equal)
+            act(R("ne32"), R("ne0"), AF.Identity, scale=32.0)
+            act(R("fo"), lanes("Wt", 0), AF.Sign)
+            bk = fil()
+            mm(P(bk, 0, L), [(R("If32"), lanes("O32", 0)), (R("NI32"), lanes("Wall", 0)), (R("NIf32"), lanes("Mt", 0))])
+            mm(P(bk, L, L), [(R("Id"), lanes("Wall", 0)), (R("NI"), tile("Wn", 0))])
+            tt(R("dM"), R("ne32"), P(bk, 0, L), OP.mult)
+            tt(R("dW"), R("ne0"), P(bk, L, L), OP.mult)
+            tt(R("dWf"), R("dW"), R("fo"), OP.mult)
+    bk = big()
+    mm(P(bk, 0, L), [(R("If"), tile("Oacc", t)) for t in (1, 2)] + [(R("NIf512"), tile("sq", t)) for t in (1, 2, 3)])
+    act(R("dM"), P(bk, 0, L), AF.Identity, bias=-3 * OACC)
+    tt(R("yob"), R("dM"), tile("Oacc", 3), OP.add)
+    add("s", "store", ("yo", "yob", 0, L), [R("yob")], [], 2000)
+    act(R("yfb"), R("Wt", 0, V), AF.Sign)
+    for q in range(8):
+        add("s", "storef", (q,), [R("yfb")], [], 2000)
+    add("s", "store", ("yx", "X", 0, V), [R("X", 0, V)], [], 3000)
+    merge(3)
+    add("s", "store", ("yx", "X", V, W), [R("X", V, W)], [], 2500)
+    return ops
+
+
+def meet(x, y):
+    if x[3] == y[3] and (x[1] - y[1]) % x[3]:
+        return False
+    return x[0] == y[0] and x[1] < y[2] and y[1] < x[2]
+
+
+ASYNC = ("load", "store", "storef", "arr")
+
+
+def link(ops):
+    hist, turn = {}, {}
+    for i, o in enumerate(ops):
+        dep, order = set(), set()
+        acc = [(x, False) for x in o["r"]] + [(x, True) for x in o["w"]]
+        for x, wr in acc:
+            for (j, y, wy) in hist.get(x[0], []):
+                if o["e"] == "t" and ops[j]["e"] == "t":
+                    order.add(j)
+                elif meet(x, y) and (wr or wy):
+                    dep.add(j)
+            if isps(x):
+                cur, prev = turn.get(x[0], ([], []))
+                if cur and ops[cur[0]]["e"] != o["e"]:
+                    cur, prev = [], cur
+                dep.update(prev)
+                turn[x[0]] = (cur + [i], prev)
+        for x, wr in acc:
+            if o["e"] == "t" and not wr:
+                if x[0] in CONST:
+                    continue
+            h = hist.setdefault(x[0], [])
+            if wr:
+                h[:] = [e for e in h if not (x[1] <= e[1][1] and e[1][2] <= x[2] and (x[3] == 1 or (x[3] == e[1][3] and meet(x, e[1]))))]
+            h.append((i, x, wr))
+        dep.discard(i)
+        order = set(j for j in order if ops[j]["w"][0][0] == o["w"][0][0] and j != i)
+        o["dep"], o["ord"] = dep, order - dep
+    for o in ops:
+        o["succ"] = []
+    for i, o in enumerate(ops):
+        for j in o["dep"] | o["ord"]:
+            ops[j]["succ"].append((i, j in o["dep"]))
+    return ops
+
+
+def cost(o, m):
+    kind, n = o["c"]
+    if kind == "u":
+        return sum(cost(x, m) for x in n)
+    if kind == "v":
+        return m[3] + m[0] * max(64, n)
+    if kind == "g":
+        return 60 + m[0] * m[1] * n
+    if kind == "p":
+        return m[2] * n
+    return n
+
+
+def lay_out(ops, seed):
+    rs = np.random.RandomState(seed)
+    n = len(ops)
+    m = MODELS[0]
+    c = [cost(o, m) for o in ops]
+    hop = m[4]
+    wob = 1 + 0.5 * rs.rand() * (rs.rand(n) - 0.5)
+    level = [0.0] * n
+    for i in range(n - 1, -1, -1):
+        level[i] = c[i] * wob[i] + max([level[j] + (hop if d else 0) for j, d in ops[i]["succ"]] + [0.0])
+    pred = [[(j, True) for j in o["dep"]] + [(j, False) for j in o["ord"]] for o in ops]
+    succ = [o["succ"] for o in ops]
+    hold = [60 if o["kind"] in ASYNC else c[i] for i, o in enumerate(ops)]
+
+    def place(order, before, back):
+        busy = {e: [] for e in "vatgsx"}
+        t0 = [0.0] * n
+        for i in order:
+            s = max([t0[j] + c[j] + (hop if d else 0) for j, d in before[i]] + [0.0])
+            off = c[i] - hold[i] if back else 0.0
+            s += off
+            b = busy[ops[i]["e"]]
+            k = len(b)
+            while k > 0 and b[k - 1][1] > s:
+                k -= 1
+            while k < len(b) and b[k][0] < s + hold[i]:
+                s = max(s, b[k][1])
+                k += 1
+            b.insert(k, (s, s + hold[i]))
+            t0[i] = s - off
+        return t0
+
+    order = sorted(range(n), key=lambda i: (-level[i], i))
+    best = None
+    for _ in range(PASSES):
+        t0 = place(order, pred, False)
+        end = max(t0[i] + c[i] for i in range(n))
+        if best is None or end < best[0]:
+            best = (end, sorted(range(n), key=lambda i: (t0[i], i)))
+        tb = place(sorted(range(n), key=lambda i: (-(t0[i] + c[i]), -i)), succ, True)
+        order = sorted(range(n), key=lambda i: (-(tb[i] + c[i]), i))
+    return best[1]
+
+
+def units(ops):
+    us, of = [], {}
+    for i, o in enumerate(ops):
+        if us and o["u"] is not None and o["u"] == ops[i - 1]["u"] and o["e"] == ops[i - 1]["e"]:
+            us[-1]["ops"].append(i)
+        else:
+            us.append(dict(e=o["e"], kind=o["kind"], ops=[i], succ=[]))
+        of[i] = len(us) - 1
+    for k, u in enumerate(us):
+        u["c"] = ("u", [ops[i] for i in u["ops"]])
+        u["dep"] = set(of[j] for i in u["ops"] for j in ops[i]["dep"]) - {k}
+        u["ord"] = set(of[j] for i in u["ops"] for j in ops[i]["ord"]) - {k} - u["dep"]
+        for j in u["dep"] | u["ord"]:
+            us[j]["succ"].append((k, j in u["dep"]))
+    return us
+
+
+def refine(us, seq, moves, seed):
+    rs = np.random.RandomState(seed)
+    n = len(us)
+    eng = ["vatgsx".index(u["e"]) for u in us]
+    dep = [tuple(u["dep"]) for u in us]
+    pre = [u["dep"] | u["ord"] for u in us]
+    cs = [[cost(u, m) for u in us] for m in MODELS]
+    hs = [[60 if u["kind"] in ASYNC else c[i] for i, u in enumerate(us)] for c in cs]
+
+    def run(sq, k):
+        c, h, hop = cs[k], hs[k], MODELS[k][4]
+        free, last = [0.0] * 6, [-1] * 6
+        t1, why = [0.0] * n, [-1] * n
+        for i in sq:
+            e = eng[i]
+            s, w = free[e], -2 - last[e]
+            for j in dep[i]:
+                if t1[j] + hop > s:
+                    s, w = t1[j] + hop, j
+            t1[i], why[i] = s + c[i], w
+            free[e], last[e] = s + h[i], i
+        return max(t1), t1, why
+
+    def score(sq):
+        r = [run(sq, k) for k in range(len(MODELS))]
+        return sum(x[0] * m[5] for x, m in zip(r, MODELS)), r
+
+    cur, r = score(seq)
+    best = (cur, seq)
+    for it in range(moves):
+        end, t1, why = r[rs.randint(len(r))]
+        i = t1.index(end)
+        arcs = []
+        while i != -1:
+            w = why[i]
+            if w <= -2:
+                w = -2 - w
+                arcs.append((w, i))
+            i = w
+        if not arcs:
+            break
+        a, b = arcs[rs.randint(len(arcs))]
+        pa, pb = seq.index(a), seq.index(b)
+        for _ in range(rs.randint(3)):
+            q = pa - 1
+            while q >= 0 and eng[seq[q]] != eng[b]:
+                q -= 1
+            if q >= 0:
+                pa = q
+        if rs.rand() < 0.5:
+            take, want = [b], set(pre[b])
+            for q in range(pb - 1, pa - 1, -1):
+                if seq[q] in want:
+                    take.append(seq[q])
+                    want |= pre[seq[q]]
+            if a in take:
+                continue
+            ts = set(take)
+            new = seq[:pa] + take[::-1] + [x for x in seq[pa:pb] if x not in ts] + seq[pb + 1:]
+        else:
+            pa = seq.index(a)
+            ts = {a}
+            for q in range(pa + 1, pb + 1):
+                if pre[seq[q]] & ts:
+                    ts.add(seq[q])
+            if b in ts:
+                continue
+            new = seq[:pa] + [x for x in seq[pa:pb + 1] if x not in ts] + [x for x in seq[pa:pb + 1] if x in ts] + seq[pb + 1:]
+        sc, r2 = score(new)
+        if sc <= cur + HEAT * (1 - it / moves) * rs.rand():
+            cur, r, seq = sc, r2, new
+            if sc < best[0]:
+                best = (sc, new)
+    return best[1]
+
+
+def plan():
+    ops = link(build())
+    us = units(ops)
+    seq = [i for u in refine(us, lay_out(us, SEED), MOVES, SEED) for i in us[u]["ops"]]
+    pos = {i: k for k, i in enumerate(seq)}
+    seen = {e: {} for e in "vatgs"}
+    need = set()
+    for i in seq:
+        o = ops[i]
+        if o["kind"] == "arr":
+            o["clock"] = {}
+            continue
+        last = {}
+        for j in o["dep"]:
+            p = ops[j]
+            key = p["e"] if p["kind"] not in ASYNC else ("d", j)
+            if key not in last or pos[j] > pos[last[key]]:
+                last[key] = j
+        o["wait"] = []
+        mine = seen[o["e"]]
+        for key, j in sorted(last.items(), key=lambda kv: -pos[kv[1]]):
+            if mine.get(key, -1) < pos[j]:
+                mine[key] = pos[j]
+                o["wait"].append(j)
+                need.add(j)
+                for k2, v in ops[j]["clock"].items():
+                    mine[k2] = max(mine.get(k2, -1), v)
+        o["clock"] = dict(mine)
+    count = {e: 0 for e in "vatg"}
+    for i in seq:
+        o = ops[i]
+        o["inc"] = i in need and o["kind"] not in ASYNC
+        if o["inc"]:
+            count[o["e"]] += 1
+            o["n"] = count[o["e"]]
+    return ops, seq, count
+
+
+_PLAN = {}
+
+
+def rank_program(g, core, T, topo):
+    rank = T.rank_of(core)
+    if rank is None:
+        return
+    if "p" not in _PLAN:
+        _PLAN["p"] = plan()
+    ops, seq, count = _PLAN["p"]
+    Q = {"v": g.vector, "a": g.scalar, "t": g.tensor, "g": g, "s": g.sync}
+    SEM = {e: T.sem["e_" + e] for e in "vatg"}
+
+    def ap(r):
+        if not isinstance(r, tuple):
+            return r
+        if r[3] == 1:
+            return T[r[0]][:, r[1]:r[2]]
+        return T[r[0]][:, r[1]:r[2]:r[3]]
+
+    stores = 0
+    for i in seq:
+        o = ops[i]
+        k, a = o["kind"], o["a"]
+        if k == "arr":
+            continue
+        q = Q[o["e"]]
+        for j in o["wait"]:
+            p = ops[j]
+            if p["kind"] == "load":
+                q.wait_ge(T.sem[p["a"][0]], 16)
+            elif p["kind"] == "arr":
+                q.wait_ge(T.sem["arr%d" % p["a"][0]], N - 1)
+            else:
+                q.wait_ge(SEM[p["e"]], p["n"])
+        ins = None
+        if k == "ts":
+            if a[5] is None:
+                ins = q.tensor_scalar(ap(a[0]), ap(a[1]), ap(a[2]), None, a[4])
+            else:
+                ins = q.tensor_scalar(ap(a[0]), ap(a[1]), ap(a[2]), ap(a[3]), a[4], a[5])
+        elif k == "tt":
+            ins = q.tensor_tensor(ap(a[0]), ap(a[1]), ap(a[2]), a[3])
+        elif k == "cp":
+            ins = q.tensor_copy(ap(a[0]), ap(a[1]))
+        elif k == "ms":
+            ins = q.memset(ap(a[0]), a[1])
+        elif k == "scan":
+            ins = q.tensor_tensor_scan(ap(a[0]), ap(a[1]), ap(a[2]), 0.0, a[3], a[4])
+        elif k == "act":
+            if a[5] is None:
+                ins = q.activation(ap(a[0]), ap(a[1]), a[2], bias=ap(a[3]), scale=ap(a[4]))
+            else:
+                ins = q.activation(ap(a[0]), ap(a[1]), a[2], bias=ap(a[3]), scale=ap(a[4]), accum_out=ap(a[5]))
+        elif k == "gat":
+            src = ap(a[1]).indirect(ap(a[2]))
+            if a[3] is not None:
+                ins = q.tensor_tensor(ap(a[0]), src, ap(a[3]), OP.add)
+            elif o["e"] == "v":
+                ins = q.tensor_copy(ap(a[0]), src)
+            else:
+                ins = q.activation(ap(a[0]), src, AF.Identity)
+        elif k == "mm":
+            ins = q.matmul(ap(a[0]), ap(a[1]), ap(a[2]), a[3], a[4])
+        elif k == "iota":
+            if SCRATCH[a[0][0]][2] == I:
+                ins = q.iota(ap(a[0]), a[1], a[2], a[3])
+            else:
+                ins = q.iota(ap(a[0]), a[1], a[2], a[3], allow_small_or_imprecise_dtypes=True)
+        elif k == "sel":
+            ins = q.affine_select(ap(a[0]), ap(a[1]), a[2], a[3], a[6], a[4], a[5])
+        elif k == "sel8":
+            ins = q.affine_select(ap(a[0]), T[a[1][0]][0:8, 0:128], a[2], a[3], 0.0, a[4], a[5])
+        elif k == "load":
+            q.dma_start(T[a[1]][:, a[3]:a[4]], T[a[2]][:, a[3]:a[4]]).then_inc(T.sem[a[0]], 16)
+        elif k == "pcp":
+            ins = q.affine_select(ap(a[0]), ap(a[1]), [[0, L]], OP.is_ge, 0.0, 0, 0)
+        elif k == "store":
+            q.dma_start(T[a[0]][:, a[2]:a[3]], T[a[1]][:, a[2]:a[3]]).then_inc(T.sem.stored, 16)
+            stores += 1
+        elif k == "storef":
+            q.dma_start(T.yf[a[0]:a[0] + 1, :], T.yfb[16 * a[0]:16 * a[0] + 1, :]).then_inc(T.sem.stored, 16)
+            stores += 1
+        elif k == "send":
+            t = a[0]
+            trs = []
+            for d in range(N - 1):
+                dst = T.cores[(rank - 1 - d) % N]
+                rid, pid = topo.addr(dst, core)
+                c = t * NS + d * G
+                trs.append(RemoteDMATransfer(dst_ids=[DstId(rid=rid, pnc=pid)], dma_engine_mask=1 << topo.engines(core, dst)[d],
+                                             remote_sem=T.sem["arr%d" % t], src=T.outb[:, c:c + G], dst=T.land[:, c:c + G]))
+            q.remote_dma_fused(trs, local_sem=T.sem.sent)
+        if o["inc"]:
+            ins.then_inc(SEM[o["e"]], 1)
+    g.wait_ge(T.sem.sent, RO * (N - 1))
+    g.sync.wait_ge(T.sem.stored, 16 * stores)

@@ -4,478 +4,608 @@ from concourse.mybir import AluOpType as OP, ActivationFunctionType as AF
 
 N, V, W, G, L, RO = 8, 1280, 1728, 64, 256, 4
 NS = (N - 1) * G
-SW = 131072.0
-CW = 1.5 * 2.0 ** 40
+SW = 65536.0
+BS = 145 * SW
+BIG = 256 * SW
 C1 = 1.5 * 2.0 ** 23
-OOWN = 90112.0
-OACC = 57856.0
-PAD = 16
+C8 = 1.5 * 2.0 ** 31
+HL = 64
 
 B, F, I, U = "bfloat16", "float32", "int32", "uint16"
+STEP = 215 / 2.0 ** 31
+SCALED = dict(NI=-1.0, N256=-256.0, P125=12544.0, N512=-512.0, NI16=-1 / 16, I16=1 / 16, I15=15.0, IBS=BS, NBS=-BS,
+              N2048=-2048.0, I2=2.0, Io=1 / 4096)
+SCALED32 = dict(If=1.0, NIf=-1.0, If16=1 / 16, Ifo=1 / 4096)
 _SB = dict(
-    ktb=(V, I), shb=(28, I), sho=(28, U), X=(W, B), O32=(V, F), Wall=(V, B), Wt=(W, B), Mt=(W, F),
-    Gw=(4096, B), A=(4096 + PAD, B), Gm=(4096, F), S=(4096, F), Gx=(4096, B), A3=(4096, B), S3=(4096, B),
-    ones=(512, B), Id=(128, B), NI=(128, B), H=(128, B), N256=(128, B), I32=(128, B), N512=(128, B), P125=(128, B),
-    Blk=(128, B), Blk0=(128, B), Sel=(2048, B), Dg=(2048, B), Dz=(17 * 128, B),
-    If=(128, F), If32=(128, F), NIf512=(128, F), on16=(128, F),
-    cst=(512, B), c16=(NS, B), cmh=(L, B), mask3=(2048, B), mask5=(NS, B), vt=(V, F),
-    pk=(16, I), pk2=(16, I), ek=(16, F), ek32=(16, F), kq=(1, F), kq2=(1, F), colh=(1, F),
-    offC=(RO * L, U), offX=(L, U), offO=(L, U), h128=(L, B), hi=(RO * L, B), lo=(RO * L, B),
-    b1=(L, F), Bi=(L, I), Mi=(L, I), lowi=(L, I), z=(RO * L, B), Wn=(RO * L, B), w17=(L, B),
-    fs=(80, I), fsb=(80, B), ths=(48, I), thf=(48, F), fo=(L, B), st=(L, B), ad=(L, B), ad2=(L, B), NI32=(128, B), NIf32=(128, F), u=(L, B), nx=(L, B), ne=(L, B), chb=(L, B), junk=(L, B),
-    Gs=(NS, B), Gh=(NS, B), cum=(NS, B), outb=(RO * NS, B), land=(RO * NS, B), rl=(NS, B),
-    acc=(512, F), Oacc=(RO * L, F), sq=(RO * L, F), cnt=(2, F), Ai=(1, I), Ai2=(1, I), acol=(1, F),
-    O0p=(L, F), dO=(L, F), ne0=(L, B), ne32=(L, B), dM=(L, F), dW=(L, B), dWf=(L, B),
-    wb3=(L, B), Op3=(L, F), yfb=(V, F), ykb=(L, F), yob=(L, F),
+    ktb=(V, I), shb=(28, I), sho=(28, U), X=(W, B), Ef=(V, F), E=(W, F),
+    Eg=(4096, F), S=(4096, F), Gx=(4096, B), A3=(4096, B), S3=(4096, B),
+    ones=(512, B), zero=(128, B), Id=(128, B), Blk=(128, B), Blk0=(128, B), NSel=(2048, B), Sel17=(2048, B), Dg=(2048, B),
+    Pk=(1024, B), Dz=(1024, B), on16=(128, F), mask3=(1024, B), mask5=(NS, B), vt=(L, F), va=(L, B), vb=(3 * L, B),
+    IdC=(128, B), IdD=(128, B), cst=(1024, B),
+    pk=(16, I), pk2=(16, I), nek=(16, F), ek=(16, F), ek12=(16, F), pc=(8, F),
+    ki=(2, I), kf=(4, F), colh=(1, F),
+    offC=(RO * L, U), offX=(L, U), offO=(L, U), w1=(L, B), wz=(RO * L, B), hq=(L, B), hi=(RO * L, B), lo=(RO * L, B),
+    b1=(L, F), ow=(RO * L, B), bh=(L, B), Wz=(RO * L, B), m16=(RO * L, F), tq=(RO * L, B), rr=(L, B), zc=(L, B), sq=(L, B),
+    acc=(512, F), h0=(L, B), bi=(L, I), mi=(L, I), Qi=(L, I), Oi=(RO * L, I),
+    fs=(80, I), fsb=(80, B), fsn=(80, B), ths=(48, I), thb=(96, B), st=(L, B), ad=(L, B), ad2=(L, B), u=(L, B), nx=(L, F), ne=(L, B),
+    chb=(L, B), junk=(L, B), Gs=(NS, B), Gh=(NS, B), cum=(NS, B), outb=(RO * NS, B), land=(RO * NS, B), rl=(NS, B),
+    cnt=(2, F), Ai=(1, I), Ai2=(1, I), acol=(1, F),
+    sc=(RO * L, F), st0=(L, B), Kn0=(L, F), dO=(L, F), ne0=(L, B), dE=(L, F), Ef3=(L, F), O3=(L, F), yfb=(V, F), ykb=(L, F), yo1=(L, F), yob=(L, F),
 )
-_S8 = dict(f8b=(V, B), th8f=(768, F), E8=(128, B), NE8=(128, F), NE8b=(128, B))
+for _n in SCALED:
+    _SB[_n] = (128, B)
+for _n in SCALED32:
+    _SB[_n] = (128, F)
 SCRATCH = {}
 for _n, (_w, _d) in _SB.items():
     SCRATCH[_n] = ("sbuf", [128, _w], _d)
-for _n, (_w, _d) in _S8.items():
-    SCRATCH[_n] = ("sbuf", [8, _w], _d)
+SCRATCH.update(Wr=("sbuf", [128, L, 16], B), Rl=("sbuf", [128, L, 17], B), f8b=("sbuf", [8, V], B), th16=("sbuf", [16, 768], B),
+               NE8=("sbuf", [8, 128], B), NEa=("sbuf", [16, 128], B), NE16=("sbuf", [16, 128], B))
 for _k in range(8):
     SCRATCH["ps%d" % _k] = ("psum", [128, 512], F)
 
-LOADS = ["l_f", "l_k0", "l_k1", "l_k2", "l_th", "l_sh", "l_x", "l_f8", "l_t8"]
+LOADS = ["l_f", "l_k0", "l_k1", "l_k2", "l_k3", "l_th", "l_sh", "l_x", "l_f8", "l_t8", "l_t9"]
 SEMAPHORES = ["e_v", "e_a", "e_t", "e_g", "stored", "sent"] + LOADS + ["arr%d" % t for t in range(RO)]
 
-MODELS = [(1.04, 1.56, 0.55, 30.0, 140.0, 1.0), (1.04, 1.15, 0.5, 20.0, 80.0, 0.5), (1.04, 1.95, 0.6, 40.0, 200.0, 0.5)]
-SEED = 1
-MOVES = 6000
-HEAT = 600.0
-PASSES = 8
-GCH = 1024
-WACT = (320, 960)
-FUSED = ((0, 0), (3, 0))
-GMV = ()
-GWV = ()
-GXV = ()
-CH = ((0, 64), (64, 128), (192, 64))
-TURNS = "A0 A0 A1 S0 A1 S0 A1 A1 S1 A2 S1 A2 S1 S1 S2 S2 X0 X0 X1 X1 X1 X1 X2 X2"
-NFIL = 2
-CONST = ("Id", "NI", "H", "N256", "I32", "N512", "P125", "Blk", "Sel", "Dg", "Dz", "If", "If32", "NIf512", "on16", "cst", "c16",
-         "cmh", "E8", "NE8", "NE8b", "NI32", "NIf32")
-ZPE = True
+MODELS = [(0.83, 1.56, 0.42, 15.0, 130.0, 1.0, 15.0, 5000.0), (0.83, 1.15, 0.42, 10.0, 100.0, 0.7, 18.0, 6500.0),
+          (0.83, 1.95, 0.42, 20.0, 160.0, 0.7, 12.0, 4000.0)]
+OPT = dict(
+    form=("d cc b",) * 4,
+    cast=("gggg", "gggg", "gggg", "gggg"),
+    small="aaa", fold=(), back=14000, gsplit=1, bits=False, rl="a", gch=1024, bh="a", wz="a", tpe=False, passes=2,
+    gat=("aaaa", "aaaa", "aaaa", "aaaa"),
+    gatx=("aaaa", "aaaa", "aaaa", "aaaa"),
+    xp=((0, 64), (64, 128), (192, 64)),
+    sp=((0, 192), (192, 64)), rp=((0, 128), (128, 128)), lov=True,
+    etab="vvva",
+    five=("aaaaa", "aaaaa", "aaaaa", "vavaa"), fil=(5, 6, 7), ahead={"x:land": 3000, "v:NSel": 3000, "g:Blk": 3000}, seed=1, turns=1, tries=300, moves=8000, heat=500.0, flight=4000, load=1.0,
+)
 
 
-def R(name, a=0, b=None, s=1):
+def shape(name):
+    return [128, 512] if name[0] == "#" else SCRATCH[name][1]
+
+
+def R(name, a=0, b=None, s=1, k0=0, k1=1):
     if b is None:
-        b = SCRATCH[name][1][1]
-    return (name, a, b, s)
+        b = shape(name)[1]
+    return (name, a, b, s, k0, k1)
 
 
 def cnt_of(r):
-    return len(range(r[1], r[2], r[3]))
-
-
-def two(r):
-    return SCRATCH[r[0]][2] in (B, U)
+    return len(range(r[1], r[2], r[3])) * (r[5] - r[4])
 
 
 def isps(r):
-    return SCRATCH[r[0]][0] == "psum"
+    return r[0][0] == "#"
 
 
-def build():
+def two(r):
+    return not isps(r) and SCRATCH[r[0]][2] in (B, U)
+
+
+def build(opt):
     ops = []
-    unit = [None]
+    unit, step = [None], [None]
 
     def add(e, kind, args, reads, writes, cost):
         ops.append(dict(e=e, kind=kind, a=args, r=[x for x in reads if isinstance(x, tuple)], w=writes,
-                        c=cost if isinstance(cost, tuple) else ("k", cost), u=unit[0]))
-
-    def vc(n, rate):
-        return ("v", n * rate)
+                        c=cost if isinstance(cost, tuple) else ("k", cost), u=unit[0], step=step[0]))
 
     def ts(out, in0, s1, op0, s2=None, op1=None):
-        add("v", "ts", (out, in0, s1, s2, op0, op1), [in0, s1, s2], [out], vc(cnt_of(out), 0.5 if two(out) and two(in0) else 1))
+        add("v", "ts", (out, in0, s1, s2, op0, op1), [in0, s1, s2], [out], ("v", cnt_of(out) * (0.5 if two(out) and two(in0) else 1)))
 
     def tt(out, a, b, op):
-        add("v", "tt", (out, a, b, op), [a, b], [out], vc(cnt_of(out), 1 if isps(a) or isps(b) else 2))
+        add("v", "tt", (out, a, b, op), [a, b], [out], ("v", cnt_of(out) * (1 if isps(a) or isps(b) else 2)))
 
     def cp(out, a):
-        add("v", "cp", (out, a), [a], [out], vc(cnt_of(out), 0.5 if two(out) and two(a) else 1))
+        add("v", "cp", (out, a), [a], [out], ("v", cnt_of(out) * (0.5 if two(out) and two(a) else 1)))
 
     def ms(out, val):
-        add("v", "ms", (out, val), [], [out], vc(cnt_of(out), 0.5 if two(out) else 1))
+        add("v", "ms", (out, val), [], [out], ("v", cnt_of(out) * (0.5 if two(out) else 1)))
 
-    def scan(out, d0, d1, op0, op1):
-        add("v", "scan", (out, d0, d1, op0, op1), [d0, d1], [out], vc(cnt_of(out), 0.5 if two(out) and two(d0) and two(d1) else 1))
+    def scan(out, d0, d1, op0, op1, first=0.0):
+        add("v", "scan", (out, d0, d1, op0, op1, first), [d0, d1], [out], ("v", cnt_of(out) * (0.5 if two(out) and two(d0) and two(d1) else 1)))
 
-    def act(out, a, func, bias=0.0, scale=1.0, accum=None):
-        add("a", "act", (out, a, func, bias, scale, accum), [a, bias, scale], [out] + ([accum] if accum else []), vc(cnt_of(out), 1))
+    def act(out, a, func=AF.Identity, bias=0.0, scale=1.0, accum=None):
+        add("a", "act", (out, a, func, bias, scale, accum), [a, bias, scale], [out] + ([accum] if accum else []), ("v", cnt_of(out)))
 
-    def gather(e, out, win, off, plus=None):
+    def lin(e, out, a, scale, bias):
+        if e == "a":
+            act(out, a, AF.Identity, bias, scale)
+        else:
+            ts(out, a, scale, OP.mult, bias, OP.add)
+
+    def gather(e, out, win, off, how=None):
         n = cnt_of(out)
-        parts = max(1, n // GCH)
-        for j in range(parts):
-            o = (out[0], out[1] + j * n // parts, out[1] + (j + 1) * n // parts, 1)
-            f = (off[0], off[1] + j * n // parts // 16, off[1] + (j + 1) * n // parts // 16, 1)
-            p = None if plus is None else (plus[0], plus[1] + j * n // parts, plus[1] + (j + 1) * n // parts, 1)
-            add(e, "gat", (o, win, f, p), [win, f, p], [o], ("g", n / parts))
+        c = min(n, opt["gch"])
+        for j in range(0, n, c):
+            o, f = R(out[0], out[1] + j, out[1] + j + c), R(off[0], off[1] + j // 16, off[1] + (j + c) // 16)
+            add(e, "gat", (o, win, f, how), [win, f], [o], ("g", c))
 
-    def mm(out, terms):
+    def sel(out, src, pattern, cmp, base, mult, fill):
+        add("g", "sel", (out, src, pattern, cmp, base, mult, fill), [src], [out], ("q", (170, cnt_of(out))))
+
+    def gcopy(out, src):
+        sel(out, src, [[0, cnt_of(out)]], OP.is_ge, 0, 0, 0.0)
+
+    def iota(out, pattern, base, mult):
+        add("g", "iota", (out, pattern, base, mult), [], [out], ("q", (130, cnt_of(out))))
+
+    def mm(out, terms, first=True, last=True):
         alone = unit[0] is None
+        run = 0
         for j, (l, r) in enumerate(terms):
-            if alone and (j % 6 == 0 or not two(l)):
-                unit[0] = len(ops)
-            add("t", "mm", (out, l, r, j == 0, j == len(terms) - 1), [l, r], [out],
-                ("p", max(64, cnt_of(out)) * (1 if two(l) else 4)))
+            c = max(64, cnt_of(out)) * (1 if two(l) else 4)
+            if alone and (j == 0 or run + c > 1100):
+                unit[0], run = len(ops), 0
+            run += c
+            add("t", "mm", (out, l, r, first and j == 0, last and j == len(terms) - 1), [l, r], [out], ("p", c))
         if alone:
             unit[0] = None
 
     def mat(name, k=0):
         return R(name, 128 * k, 128 * k + 128)
 
-    def P(bank, a, n):
-        return R("ps%d" % bank, a, a + n)
+    banks = [0]
 
-    rot = [0]
+    def bank(kind="c"):
+        banks[0] += 1
+        return "#%s%d" % (kind, banks[0])
 
-    def big():
-        rot[0] += 1
-        return NFIL + (rot[0] - 1) % (6 - NFIL)
+    def P(bk, a, n):
+        return R(bk, a, a + n)
 
-    rot2 = [0]
+    def one(n):
+        return R("ones", 0, n)
 
-    def fil():
-        rot2[0] += 1
-        return (rot2[0] - 1) % NFIL
+    def dma(e, sem, dst, src, cost, reads=()):
+        add(e, "load", (sem, dst, src), list(reads), [dst], cost * opt["load"])
 
-    add("s", "load", ("l_k0", "ktb", "kt", 0, 320), [], [R("ktb", 0, 320)], 2600)
-    add("a", "load", ("l_k1", "ktb", "kt", 320, 640), [], [R("ktb", 320, 640)], 3000)
-    add("s", "load", ("l_k2", "ktb", "kt", 640, V), [], [R("ktb", 640, V)], 3600)
-    add("a", "load", ("l_f", "fs", "f0", None, None), [], [R("fs")], 3000)
-    add("s", "load", ("l_th", "ths", "th", None, None), [], [R("ths")], 3600)
-    add("s", "load", ("l_sh", "shb", "shw", 0, 28), [], [R("shb")], 2200)
-    add("s", "load", ("l_x", "X", "x0", 0, W), [], [R("X")], 4000)
+    cuts = (0, 320, 640, 960, V)
+    for j in range(4):
+        dma("sa"[j % 2], "l_k%d" % j, R("ktb", cuts[j], cuts[j + 1]), ("kt", cuts[j], cuts[j + 1]), 1800 + 200 * j)
+    dma("a", "l_f", R("fs"), ("f0", None, None), 1700)
+    dma("s", "l_th", R("ths"), ("th", None, None), 2600)
+    dma("s", "l_sh", R("shb"), ("shw", None, None), 2600)
+    dma("s", "l_x", R("X"), ("x0", None, None), 3200)
     ms(R("ones"), 1.0)
-    add("g", "iota", (R("pk"), [[-1, 16]], 16, 1), [], [R("pk")], 200)
-    add("g", "sel", (R("Id"), mat("ones"), [[-1, 128]], OP.is_equal, 0, 1, 0.0), [R("ones")], [R("Id")], 430)
-    add("g", "sel", (R("Blk0"), mat("ones"), [[-16, 8], [0, 16]], OP.is_ge, 0, 1, 0.0), [R("ones")], [R("Blk0")], 430)
-    add("g", "sel", (R("Blk"), R("Blk0"), [[16, 8], [0, 16]], OP.is_ge, 15, -1, 0.0), [R("Blk0")], [R("Blk")], 430)
-    add("g", "sel8", (R("E8"), R("ones"), [[1, 8], [0, 16]], OP.is_equal, 0, -1), [R("ones")], [R("E8")], 430)
-    add("g", "iota", (R("vt"), [[1, V]], int(-OOWN), 0), [], [R("vt")], 2700)
+    ms(R("zero"), 0.0)
+    iota(R("pk"), [[-1, 16]], 16, 1)
+    sel(R("Blk0"), one(128), [[-16, 8], [0, 16]], OP.is_ge, 0, 1, 0.0)
+    sel(R("Blk"), R("Blk0"), [[16, 8], [0, 16]], OP.is_ge, 15, -1, 0.0)
+    sel(R("Id"), one(128), [[-1, 128]], OP.is_equal, 0, 1, 0.0)
+    sel(R("NE8"), R("zero"), [[1, 8], [0, 16]], OP.not_equal, 0, -1, -1.0)
+    sel(R("NEa"), R("zero"), [[1, 8], [0, 16]], OP.not_equal, 0, -1, -1.0)
+    sel(R("NE16"), R("NEa"), [[1, 8], [0, 16]], OP.not_equal, 8, -1, -1.0)
+    sel(R("IdC"), R("Id"), [[-1, 128]], OP.not_equal, -1, 1, STEP)
+    sel(R("IdD"), R("IdC"), [[-1, 128]], OP.not_equal, 127, 1, STEP)
+    ms(R("cst"), 1.0)
+    ms(R("cst", 0, 1024, 16), -2 * BIG)
+    iota(R("vt"), [[5, L]], 0, 0)
+    iota(R("va"), [[160, 8], [0, 32]], 0, 0)
+    iota(R("vb"), [[1, 3], [0, 8], [5, 32]], 0, 0)
+    iota(R("mask5"), [[0, N - 1], [G, G]], 8, 0)
+    act(R("mask3"), R("cst"), AF.Relu, scale=256.0)
     ts(R("pk2"), R("pk"), 15, OP.bitwise_and)
+    ts(R("nek"), R("pk2"), 0.0, OP.is_equal, -1.0, OP.mult)
     ts(R("ek"), R("pk2"), 0.0, OP.is_equal)
-    ts(R("ek32"), R("ek"), -32.0, OP.mult)
-    ts(R("kq"), R("pk2", 0, 1), -7.5, OP.add)
-    tt(R("kq2"), R("kq"), R("kq"), OP.mult)
-    ts(R("colh"), R("kq2"), -2048.0, OP.mult, 512.0 + 57344.0 - 32768.0, OP.add)
-    for nm, val in (("NI", -1.0), ("H", 0.5), ("N256", -256.0), ("I32", 1 / 32), ("N512", -512.0), ("P125", 12544.0),
-                    ("If", 1.0), ("If32", 1 / 32), ("NIf512", -512.0), ("NI32", -1 / 32), ("NIf32", -1 / 32)):
-        ts(R(nm), R("Id"), val, OP.mult)
-    ts(R("NE8"), R("E8"), -1.0, OP.mult)
-    ts(R("NE8b"), R("E8"), -1.0, OP.mult)
+    ts(R("ek12"), R("ek"), 1 / 4096, OP.mult)
+    tt(R("pc"), R("ek", 0, 16, 2), R("ek12", 1, 16, 2), OP.add)
+    ki, kf = [R("ki", j, j + 1) for j in range(2)], [R("kf", j, j + 1) for j in range(4)]
+    ts(ki[0], R("pk2", 0, 1), 1, OP.logical_shift_right)
+    ts(kf[0], ki[0], -3.5, OP.add)
+    tt(kf[1], kf[0], kf[0], OP.mult)
+    ts(ki[1], R("pk2", 0, 1), 1, OP.bitwise_and)
+    ts(kf[2], ki[1], 2048.0, OP.mult, -2048.0, OP.add)
+    tt(kf[3], kf[1], kf[2], OP.mult)
+    ts(R("colh"), kf[3], -32768.0, OP.add)
+    for nm, val in SCALED.items():
+        if nm in ("NI", "NI16", "I15"):
+            ts(R(nm), R("Id"), val, OP.mult)
+        else:
+            sel(R(nm), R("zero"), [[-1, 128]], OP.not_equal, 0, 1, val)
+    for nm, val in SCALED32.items():
+        act(R(nm), R("Id"), scale=val)
     for k in range(16):
-        act(mat("Sel", k), R("Blk"), AF.Identity, scale=R("ek", k, k + 1))
-        if k % 2:
-            ts(mat("Dg", k), R("Id"), R("ek32", k, k + 1), OP.mult)
-        else:
-            act(mat("Dg", k), R("Id"), AF.Identity, scale=R("ek32", k, k + 1))
-    for k in range(17):
-        ts(mat("Dz", k), R("Id"), 1024.0 * (2 * (k - 1) - 15), OP.mult)
+        ts(mat("NSel", k), R("Blk"), R("nek", k, k + 1), OP.mult)
+    for k in range(2):
+        sel(R("Dg", 1024 * k, 1024 * k + 1024), R("NSel", 1024 * k, 1024 * k + 1024), [[0, 8], [-1, 128]], OP.is_equal, 0, 1, 0.0)
+        act(R("Sel17", 1024 * k, 1024 * k + 1024), R("NSel", 1024 * k, 1024 * k + 1024), scale=-17 / SW)
+    for j in range(8):
+        ts(mat("Pk", j), R("Blk"), R("pc", j, j + 1), OP.mult)
+    for j in range(8):
+        sel(mat("Dz", j), R("zero"), [[-1, 128]], OP.not_equal, 0, 1, 4096.0 * (j - 3.5))
     ms(R("on16"), 1 / 16)
-    ms(R("c16"), 16.0)
-    ms(R("cmh"), -0.5)
-    add("g", "sel", (R("cst"), R("ones"), [[0, 32], [1, 16]], OP.is_gt, 0, 0, -2.0 ** 22), [R("ones")], [R("cst")], 1300)
-    add("g", "iota", (R("mask3"), [[0, 128], [256, 16]], 0, 0), [], [R("mask3")], 4500)
-    add("g", "iota", (R("mask5"), [[0, N - 1], [G, G]], 0, 0), [], [R("mask5")], 1100)
-    ms(R("A", 0, PAD), 0.0)
-    ms(R("Wt", V, W), 0.0)
-    ms(R("Mt", V, W), 0.0)
+    ms(R("Rl", 0, L, 1, 0, 1), 2 * BIG)
+    ms(R("E", V, W), 0.0)
     ms(R("cnt"), 0.0)
+    ts(R("fsn"), R("fs"), -BIG, OP.mult)
     cp(R("fsb"), R("fs"))
-    cp(R("thf"), R("ths"))
-    add("s", "load", ("l_f8", "f8b", "fsb", None, None), [R("fsb")], [R("f8b")], 2200)
-    add("s", "load", ("l_t8", "th8f", "thf", None, None), [R("thf")], [R("th8f")], 2200)
+    ts(R("thb", 0, 48), R("ths"), C8, OP.add, C8, OP.subtract)
+    tt(R("thb", 48, 96), R("ths"), R("thb", 0, 48), OP.subtract)
+    dma("s", "l_f8", R("f8b"), ("fsb", None, None), 1600, [R("fsb")])
+    add("s", "load16", ("l_t8", 0), [R("thb", 0, 48)], [R("th16", 0, 768, 1, 0, 1)], 1600)
+    add("s", "load16", ("l_t9", 1), [R("thb", 48, 96)], [R("th16", 0, 768, 1, 1, 2)], 1600)
     cp(R("sho"), R("shb"))
-    for a, b in ((0, 320), (320, 640), (640, 960), (960, V)):
-        ts(R("O32", a, b), R("ktb", a, b), 32.0, OP.mult, SW, OP.add)
-        if a in WACT:
-            act(R("Gw", a, b), R("O32", a, b), AF.Identity, bias=128.0, scale=1 / SW)
-            act(R("Wall", a, b), R("Gw", a, b), AF.Identity, bias=-128.0 * SW, scale=SW)
+    for j in range(4):
+        a, b = cuts[j], cuts[j + 1]
+        ts(R("Ef", a, b), R("ktb", a, b), 16.0, OP.mult, BS, OP.add)
+        bk = bank()
+        if opt["etab"][j] == "v":
+            for q in range(4):
+                mm(P(bk, 80 * q, 80), [(mat("NSel", a // 80 + q), R("fsn"))])
+            tt(R("E", a, b), R("Ef", a, b), P(bk, 0, b - a), OP.min)
         else:
-            ts(R("Wall", a, b), R("O32", a, b), CW, OP.add, CW, OP.subtract)
-        bk = big()
-        mm(P(bk, 0, b - a), [(R("If"), R("O32", a, b)), (R("NI"), R("Wall", a, b))])
-        act(R("Mt", a, b), P(bk, 0, b - a), AF.Identity)
-        bk = fil()
-        for q in range(4):
-            mm(P(bk, 80 * q, 80), [(mat("Sel", a // 80 + q), R("fsb"))])
-        tt(R("Wt", a, b), R("Wall", a, b), P(bk, 0, b - a), OP.mult)
+            mm(P(bk, 0, b - a), [(R("If"), R("Ef", a, b))], True, False)
+            for q in range(4):
+                mm(P(bk, 80 * q, 80), [(mat("NSel", a // 80 + q), R("fsn"))], False, q == 3)
+            act(R("E", a, b), P(bk, 0, b - a), AF.Relu, bias=-BIG)
 
-    def lanes(name, m, h=None):
-        if h is None:
-            return R(name, m, V, 5)
-        return R(name, m + 5 * CH[h][0], 5 * (CH[h][0] + CH[h][1]), 5)
+    def lanes(name, m, a=0, n=L):
+        return R(name, m + 5 * a, 5 * (a + n), 5)
 
-    def tile(name, t, h=None):
-        if h is None:
-            return R(name, t * L, t * L + L)
-        return R(name, t * L + CH[h][0], t * L + CH[h][0] + CH[h][1])
+    def tile(name, t, a=0, n=L):
+        return R(name, t * L + a, t * L + a + n)
 
-    def wide(name, h, pad=0):
-        return R(name, pad + 16 * CH[h][0], pad + 16 * (CH[h][0] + CH[h][1]))
+    def own(t, a=0, n=L):
+        return lanes("Ef", t, a, n) if t < 3 else R("Ef3", a, a + n)
 
-    def prep_off(t):
-        ts(tile("offC", t), lanes("Mt", t % 3), 1 / 32, OP.mult)
+    def prep(t, a=0, n=L):
+        bk = bank("c" if t in (0, 3) else "f")
+        y, w1, hq = P(bk, 0, n), tile("w1", 0, a, n), tile("hq", 0, a, n)
+        act(w1, own(t, a, n))
+        mm(y, [(R("If16"), own(t, a, n)), (R("NI16"), w1)])
+        cp(tile("offC", t, a, n), y)
+        lin("v" if t in (0, 3) else opt["small"][0], tile("wz", t, a, n), w1, 1.0, -BS)
+        act(hq, y, bias=32768.0)
+        lin(opt["small"][1], tile("hi", t, a, n), hq, 1.0, R("colh"))
+        if opt["lov"]:
+            ts(tile("h0", 0, a, n), hq, -32768.0, OP.add)
+            tt(tile("lo", t, a, n), y, tile("h0", 0, a, n), OP.subtract)
+        else:
+            y = P(bank("f"), 0, n)
+            mm(y, [(R("If16"), own(t, a, n)), (R("NI16"), w1), (R("NI"), hq)])
+            act(tile("lo", t, a, n), y, bias=32768.0)
 
-    def prep_pieces(t):
-        m = t % 3
-        act(R("h128"), lanes("Mt", m), AF.Identity, bias=128.0, scale=1 / 8192)
-        act(tile("hi", t), R("h128"), AF.Identity, bias=R("colh"), scale=256.0)
-        bk = fil()
-        mm(P(bk, 0, L), [(R("If32"), lanes("Mt", m)), (R("N256"), R("h128"))])
-        act(tile("lo", t), P(bk, 0, L), AF.Identity, bias=32768.0)
+    def step2(t, a, HL, form):
+        o, per = 16 * a, 512 // HL
+        based = form in "ad"
+        wz = tile("wz", t, a, HL)
+        for c in range(a, a + HL, 64):
+            gather(opt["gat"][t][c // 64], R("Eg", 16 * c, 16 * c + 1024), R("E"), tile("offC", t, c, 64))
 
-    def gm(t, h):
-        if (t, h) not in FUSED:
-            gather("v" if (t, h) in GMV else "a", wide("Gm", h), R("Mt"), tile("offC", t, h))
+        def relu(out, src):
+            if based:
+                ts(out, src, BS, OP.max)
+            else:
+                act(out, src, AF.Relu, bias=-BS)
 
-    def origin(t, oprev):
-        act(tile("sq", t), tile("z", t), AF.Square)
-        for j in range(8):
-            bk = fil()
-            for q in range(2):
-                k = 2 * j + q
-                mm(P(bk, L * q, L), [(mat("Sel", k), tile("hi", t)), (mat("Sel", k), tile("lo", t)), (mat("Dz", k + 1), tile("z", t))])
-            if j == 0:
-                act(R("acc"), P(bk, 0, 512), AF.Identity)
+        if form in "de":
+            for k0 in range(0, 16, per):
+                bk = bank()
+                unit[0] = len(ops)
+                for k in range(per):
+                    mm(P(bk, HL * k, HL), [(mat("NSel", k0 + k), wz)])
+                for k in range(per):
+                    tt(R("Wr", a, a + HL, 1, k0 + k, k0 + k + 1), R("Eg", o + k0 + k, o + 16 * HL, 16), P(bk, HL * k, HL), OP.add)
+                unit[0] = None
+            for c in range(a, a + HL, 64):
+                relu(R("Rl", c, c + 64, 1, 1, 17), R("Wr", c, c + 64, 1, 0, 16))
+        else:
+            n = 64 // opt["gsplit"]
+            for c in range(a, a + HL, n):
+                if opt["cast"][t][c // 64] == "g":
+                    gcopy(R("Wr", c, c + n, 1, 0, 16), R("Eg", 16 * c, 16 * (c + n)))
+                else:
+                    act(R("Wr", c, c + n, 1, 0, 16), R("Eg", 16 * c, 16 * (c + n)))
+            for k0 in range(0, 16, per):
+                bk = bank()
+                unit[0] = len(ops)
+                if form == "c":
+                    for k in range(per):
+                        mm(P(bk, HL * k, HL), [(mat("NSel", k0 + k), wz), (R("Id"), R("Wr", a, a + HL, 1, k0 + k, k0 + k + 1))])
+                    relu(P(bk, 0, 512), P(bk, 0, 512))
+                    for k in range(per):
+                        ek = R("Eg", o + k0 + k, o + 16 * HL, 16)
+                        tt(ek, ek, P(bk, HL * k, HL), OP.subtract)
+                    unit[0] = None
+                    continue
+                mm(P(bk, 0, 512), [(R("Id"), R("Wr", a, a + HL, 1, k0, k0 + per))], True, False)
+                for k in range(per):
+                    mm(R(bk, k, 512, per), [(mat("NSel", k0 + k), wz)], False, k == per - 1)
+                unit[0] = None
+                relu(R("Rl", a, a + HL, 1, k0 + 1, k0 + per + 1), P(bk, 0, 512))
+        for c in range(o, o + 16 * HL, 1024) if form == "c" else ():
+            scan(R("S", c, c + 1024), R("cst"), R("Eg", c, c + 1024), OP.add, OP.max)
+        for c in range(0, HL, 32) if form != "c" else ():
+            bk = bank()
+            if not based:
+                mm(P(bk, 0, 512), [(R("Id"), one(512))], True, False)
+            mm(P(bk, 0, 512), [(R("IdD" if based else "Id"), R("Rl", a + c, a + c + 32, 1, 1, 17)),
+                               (R("NI"), R("Rl", a + c, a + c + 32, 1, 0, 16))], based, True)
+            scan(R("S", o + 16 * c, o + 16 * c + 512), P(bk, 0, 512), R("Eg", o + 16 * c, o + 16 * c + 512), OP.add, OP.max)
+
+    def rival(t, pieces):
+        bk, a0, n = bank(), pieces[0][0], sum(w[1] for w in pieces)
+        calls = [(P(bk, 0, n), [(R("If"), own(t, a0, n)), (R("I15"), one(n))]
+                  + [(mat("Dg", k), R("Wr", a0, a0 + n, 1, k, k + 1)) for k in range(16)])]
+        for a, HL, form in pieces:
+            more = ([(R("NI"), tile("wz", t, a, HL))] if form in "de" else []) + ([(R("NBS"), one(HL))] if form in "ad" else [])
+            more += [(R("Id"), R("Rl", a, a + HL, 1, 16, 17))] if form != "c" else []
+            if more:
+                calls.append((P(bk, a - a0, HL), more))
+        for j, (out, terms) in enumerate(calls):
+            mm(out, terms, j == 0, j == len(calls) - 1)
+        for a, HL, form in pieces:
+            winner(t, a, HL, form, P(bk, a - a0, HL), P(bk, 128 + a - a0, HL), P(bk, 256 + a - a0, HL))
+
+    def winner(t, a, HL, form, p1, wp, q):
+        o, based = 16 * a, form in "ad"
+        r15, s15 = R("Rl", a, a + HL, 1, 16, 17), R("S", o + 15, o + 16 * HL, 16)
+        b1, bh = R("b1", a, a + HL), R("bh", a, a + HL)
+        if opt["bits"]:
+            bi, mi = R("bi", a, a + HL), R("mi", a, a + HL)
+            tt(bi, s15, p1, OP.max)
+            ts(mi, bi, 4, OP.logical_shift_right, 2047, OP.bitwise_and)
+            cp(R("offX", a, a + HL), mi)
+            tt(tile("ow", t, a, HL), s15, p1, OP.is_gt)
+            cp(bh, bi)
+            if based:
+                tt(tile("Wz", t, a, HL), bh, r15, OP.subtract)
+            elif form == "c":
+                lin(opt["wz"], tile("Wz", t, a, HL), bh, 1.0, -BS)
+            else:
+                mm(wp, [(R("Id"), bh), (R("NI"), r15)])
+                lin(opt["wz"], tile("Wz", t, a, HL), wp, 1.0, -BS)
+            return
+        tt(b1, s15, p1, OP.max)
+        if opt["bh"] == "a":
+            act(bh, b1)
+        else:
+            cp(bh, b1)
+        tt(tile("ow", t, a, HL), s15, p1, OP.is_gt)
+        mm(q, [(R("If"), b1), (R("NI"), bh)])
+        if form != "c":
+            mm(wp, [(R("Id"), bh), (R("NI"), r15)])
+        ts(R("offX", a, a + HL), q, 1 / 16, OP.mult, -15 / 32, OP.add)
+        if form != "c":
+            lin(opt["wz"], tile("Wz", t, a, HL), wp, 1.0, 0.0 if based else -BS)
+        else:
+            lin(opt["wz"], tile("Wz", t, a, HL), bh, 1.0, -BS)
+        if not opt["tpe"]:
+            ts(tile("m16", t, a, HL), R("offX", a, a + HL), 16.0, OP.mult)
+            tt(tile("tq", t, a, HL), tile("m16", t, a, HL), q, OP.subtract)
+
+    def step3(t, a, n):
+        o = 16 * a
+        for c in range(0, n, HL):
+            gather(opt["gatx"][t][(a + c) // HL], R("Gx", o + 16 * c, o + 16 * (c + HL)), R("X"), R("offX", a + c, a + c + HL))
+        per = 512 // n
+        for k0 in range(0, 16, per):
+            bk = bank()
+            unit[0] = len(ops)
+            for k in range(per):
+                mm(P(bk, n * k, n), [(mat("Sel17", k0 + k), tile("Wz", t, a, n))])
+            for k in range(per):
+                tt(R("A3", o + k0 + k, o + 16 * n, 16), R("Gx", o + k0 + k, o + 16 * n, 16), P(bk, n * k, n), OP.min)
+            unit[0] = None
+        for c in range(o, o + 16 * n, 1024):
+            scan(R("S3", c, c + 1024), R("mask3"), R("A3", c, c + 1024), OP.min, OP.max)
+
+    def origin(t, prev):
+        bk = bank("f")
+        y = P(bk, 0, L)
+        if opt["tpe"]:
+            terms = [(R("If"), R("b1")), (R("NI"), R("bh")), (R("NIf"), tile("m16", t)), (R("NI"), tile("ow", t))]
+        else:
+            terms = [(R("NI"), tile("tq", t)), (R("NI"), tile("ow", t))]
+        mm(y, terms)
+        act(R("rr"), y, scale=-0.5, bias=198.75)
+        y = P(bk, L, L)
+        mm(y, terms + [(R("I2"), R("rr"))])
+        lin(opt["small"][2], R("zc"), R("rr"), 1.0, -195.5)
+        act(R("sq"), R("rr"), AF.Square, bias=-195.5)
+        act(tile("sc", t), y, scale=-4095.0, bias=4095.0 * 398 + 1)
+        fold = t in opt["fold"]
+        for j in range(0, 8, 2):
+            bk = bank("f")
+            for i in range(2):
+                mm(P(bk, L * i, L), [(mat("Dz", j + i), R("zc")), (R("N2048"), R("sq")),
+                                     (mat("Pk", j + i), tile("hi", t)), (mat("Pk", j + i), tile("lo", t))])
+            if fold:
+                act(R("cands", (9 * t + j) * L, (9 * t + j + 2) * L), P(bk, 0, 512))
+            elif j == 0:
+                act(R("acc"), P(bk, 0, 512))
             else:
                 tt(R("acc"), R("acc"), P(bk, 0, 512), OP.max)
-        bk = fil()
-        mm(P(bk, 0, L), [(R("If"), oprev), (mat("Dz", 0), tile("z", t))])
+        bk = bank("f")
+        mm(P(bk, 0, L), [(R("N2048"), tile("ow", t))] + prev)
+        if fold:
+            act(tile("cands", 9 * t + 8), P(bk, 0, L))
+            add("g", "fold", (t,), [R("cands", 9 * t * L, 9 * (t + 1) * L)], [R("folded", t, t + 1)], 500)
+            add("x", "back", (t,), [R("folded", t, t + 1)], [tile("pick", t)], opt["back"])
+            tt(R("Qi"), tile("sc", t), tile("pick", t), OP.mult)
+            ts(tile("Oi", t), R("Qi"), 4095, OP.bitwise_and)
+            return
         tt(P(bk, L, L), R("acc", 0, L), P(bk, 0, L), OP.max)
-        tt(tile("Oacc", t), R("acc", L, 512), P(bk, L, L), OP.max)
+        tt(P(bk, 0, L), R("acc", L, 512), P(bk, L, L), OP.max)
+        tt(R("Qi"), tile("sc", t), P(bk, 0, L), OP.mult)
+        ts(tile("Oi", t), R("Qi"), 4095, OP.bitwise_and)
 
     def merge(t):
         ld = R("land", t * NS, t * NS + NS)
-        add("x", "arr", (t,), [R("outb", t * NS, t * NS + NS)], [ld], 9000)
-        act(R("rl"), ld, AF.Relu, bias=1.0)
-        mm(P(7, 0, NS), [(R("Id"), R("X", V, W)), (R("N256"), R("rl"))])
-        tt(R("X", V, W), ld, P(7, 0, NS), OP.max)
+        add("x", "arr", (t,), [R("sent", t, t + 1)], [ld], ("f", 0))
+        if opt["rl"] == "a":
+            act(R("rl"), ld, AF.Relu, bias=1.0)
+        else:
+            ts(R("rl"), ld, 1.0, OP.add, 0.0, OP.max)
+        bk = bank()
+        mm(P(bk, 0, NS), [(R("Id"), R("X", V, W))], True, False)
+        mm(P(bk, 0, NS), [(R("N256"), R("rl"))], False, True)
+        tt(R("X", V, W), ld, P(bk, 0, NS), OP.max)
 
-    prep_off(0)
-    gm(0, 0)
+    prep(0)
     for t in range(RO):
         m = t % 3
         if t == 3:
-            b1, b2, b3 = big(), big(), big()
-            for h in range(2):
-                gather("av"[h], R("Gx", 2048 * h, 2048 * h + 2048), R("Wt"), R("offO", 128 * h, 128 * h + 128))
-                mm(P(b1, 128 * h, 128), [(mat("Dg", k), R("Gx", 2048 * h + k, 2048 * h + 2048, 16)) for k in range(16)])
-            fr = P(b2, 0, L)
-            act(fr, P(b1, 0, L), AF.Relu, bias=1.0)
-            tt(P(b1, 0, L), R("dM"), fr, OP.mult)
-            tt(P(b1, L, L), R("dWf"), fr, OP.mult)
-            tt(lanes("Mt", 0), lanes("Mt", 0), P(b1, 0, L), OP.add)
-            tt(lanes("Wt", 0), lanes("Wt", 0), P(b1, L, L), OP.add)
-            prep_off(3)
-            tt(P(b3, 0, L), R("dW"), fr, OP.mult)
-            tt(P(b3, L, L), R("dO"), fr, OP.mult)
-            tt(R("wb3"), tile("Wn", 0), P(b3, 0, L), OP.add)
-            tt(R("Op3"), R("O0p"), P(b3, L, L), OP.add)
-            gm(3, 0)
-        if t in (0, 3):
-            prep_pieces(t)
-        for h in range(len(CH)):
-            gather("v" if (t, h) in GWV else "a", wide("Gw", h), R("Wt"), tile("offC", t, h))
-        for h in range(1, len(CH)):
-            gm(t, h)
-
-        def clamp(out, pad, src, wts, h):
-            o, n = 16 * CH[h][0], CH[h][1]
-            per = min(16, 512 // n)
-            for k0 in range(0, 16, per):
-                bk = big()
-                ks = range(k0, min(16, k0 + per))
-                unit[0] = len(ops)
-                for k in ks:
-                    mm(P(bk, n * (k - k0), n), [(mat("Sel", k), wts)])
-                for k in ks:
-                    tt(R(out, pad + o + k, pad + o + 16 * n, 16), R(src, o + k, o + 16 * n, 16), P(bk, n * (k - k0), n), OP.min)
-                unit[0] = None
-                if k0 + per < 16:
-                    yield
-
-        def step2a(h):
-            yield from clamp("A", PAD, "Gw", lanes("Wall", m, h) if t < 3 else tile("wb3", 0, h), h)
-            yield
-
-        def step2b(h):
-            wb = lanes("Wall", m, h) if t < 3 else tile("wb3", 0, h)
-            o, n = 16 * CH[h][0], CH[h][1]
-            fused = (t, h) in FUSED
-            if fused:
-                gather("v", wide("Gm", h), R("Mt"), tile("offC", t, h), wide("A", h, PAD))
-            for a in range(o, o + 16 * n, 512):
-                if a > o:
-                    yield
-                if fused:
-                    scan(R("S", a, a + 512), R("cst"), R("Gm", a, a + 512), OP.add, OP.max)
-                    continue
-                bk = big()
-                mm(P(bk, 0, 512), [(R("Id"), R("cst")), (R("Id"), R("A", PAD + a - 1, PAD + a + 511)), (R("NI"), R("A", PAD + a, PAD + a + 512))])
-                scan(R("S", a, a + 512), P(bk, 0, 512), R("Gm", a, a + 512), OP.add, OP.max)
-            a15 = R("A", PAD + o + 15, PAD + o + 16 * n, 16)
-            s15 = R("S", o + 15, o + 16 * n, 16)
-            p1, p3 = P(6, o // 8, n), P(6, o // 8 + n, n)
-            own = [(R("If"), lanes("O32", m, h))] if t < 3 else [(R("If"), lanes("Mt", m, h)), (R("Id"), wb)]
-            mm(p1, own + [(R("Id"), R("c16", 0, n))] + [(mat("Dg", k), R("Gw", o + k, o + 16 * n, 16)) for k in range(16)]
-               + ([] if fused else [(R("NI"), a15)]))
-            if fused:
-                tt(tile("Bi", 0, h), s15, p1, OP.max)
-            else:
-                mm(p3, [(R("Id"), a15)])
-                tt(tile("b1", 0, h), s15, p1, OP.max)
-                tt(tile("Bi", 0, h), tile("b1", 0, h), p3, OP.add)
-            ts(tile("Mi", 0, h), tile("Bi", 0, h), 5, OP.logical_shift_right, 4095, OP.bitwise_and)
-            cp(tile("offX", 0, h), tile("Mi", 0, h))
-            ts(tile("Wn", t, h), tile("Bi", 0, h), CW, OP.add, CW, OP.subtract)
-            act(tile("w17", 0, h), tile("Wn", t, h), AF.Identity, bias=-17.0, scale=17 / SW)
-            if h < len(CH) - 1:
-                yield
-                return
-            ts(lanes("Mt", m), R("Mi"), 32.0, OP.mult)
-            if any((t, j) in FUSED for j in range(len(CH))) or not ZPE:
-                ts(R("lowi"), R("Bi"), 31, OP.bitwise_and)
-                ts(tile("z", t), R("lowi"), -2.0, OP.mult, 15.0, OP.add)
-            else:
-                bk = fil()
-                mm(P(bk, 0, L), [(R("If32"), R("b1")), (R("I32"), R("A", PAD + 15, PAD + 4096, 16)),
-                                 (R("NI32"), tile("Wn", t)), (R("NIf32"), lanes("Mt", m))])
-                act(tile("z", t), P(bk, 0, L), AF.Identity, bias=15.0, scale=-64.0)
-            yield
-
-        def step3(h):
-            if h == 0 and t > 0:
-                merge(t - 1)
-            gather("v" if (t, h) in GXV else "a", wide("Gx", h), R("X"), tile("offX", 0, h))
-            yield from clamp("A3", 0, "Gx", tile("w17", 0, h), h)
-            scan(wide("S3", h), R("mask3", 0, 16 * CH[h][1]), wide("A3", h), OP.min, OP.max)
-            yield
-
-        work = {}
-        for w in TURNS.split():
-            if w not in work:
-                work[w] = {"A": step2a, "S": step2b, "X": step3}[w[0]](int(w[1]))
-            next(work[w])
-        assert len(work) == 3 * len(CH) and all(next(w, 1) == 1 for w in work.values())
+            for h in range(4):
+                gather("av"[h % 2], R("Gx", 1024 * h, 1024 * h + 1024), R("E"), R("offO", HL * h, HL * h + HL), "sign")
+            for a, n in opt["rp"]:
+                bk = bank()
+                fr, tk, s0 = P(bk, 0, n), P(bk, 128, n), P(bk, 256, n)
+                mm(s0, [(R("Id"), tile("st0", 0, a, n))])
+                mm(fr, [(R("Id"), one(n))] + [(mat("Dg", k), R("Gx", 16 * a + k, 16 * (a + n), 16)) for k in range(16)])
+                tt(tk, tile("dE", 0, a, n), fr, OP.mult)
+                tt(tile("Ef3", 0, a, n), tile("Kn0", 0, a, n), tk, OP.add)
+                tt(lanes("E", 0, a, n), tile("Ef3", 0, a, n), s0, OP.mult)
+                tt(tk, tile("dO", 0, a, n), fr, OP.mult)
+                tt(tile("O3", 0, a, n), tile("Oi", 0, a, n), tk, OP.add)
+                prep(3, a, n)
+        step[0] = (t, 2)
+        a = 0
+        for word in opt["form"][t].split():
+            pieces = []
+            for w in word:
+                pieces.append((a, 128 if w.isupper() else 64, w.lower()))
+                step2(t, *pieces[-1])
+                a += pieces[-1][1]
+            rival(t, pieces)
+        step[0] = None
+        if opt["tpe"] or opt["bits"]:
+            lin("v", tile("m16", t), R("offX"), 16.0, 0.0)
+        if opt["bits"]:
+            ts(R("mi"), R("bi"), 15, OP.bitwise_and)
+            ts(tile("tq", t), R("mi"), -1.0, OP.mult)
+        if t > 0:
+            merge(t - 1)
+        step[0] = (t, 3)
+        for a, n in opt["xp"]:
+            step3(t, a, n)
+        step[0] = None
         if t < 2:
-            prep_off(t + 1)
-            prep_pieces(t + 1)
-            gm(t + 1, 0)
+            prep(t + 1)
         if t == 3:
-            bk = fil()
-            mm(P(bk, 0, L), [(R("I32"), tile("Wn", j)) for j in (1, 2, 3)] + [(R("If32"), lanes("Mt", j)) for j in range(3)])
-            act(R("ykb"), P(bk, 0, L), AF.Identity, bias=-3 * 4096.0)
-            add("s", "store", ("yk", "ykb", 0, L), [R("ykb")], [], 2000)
-            origin(3, R("Op3"))
-        y = R("S3", 15, 4096, 16)
-        x = lanes("X", m)
-        mm(P(6, L, L), [(R("Id"), tile("Wn", t))])
-        mm(P(6, 0, L), [(R("NI"), x), (R("Id"), y)])
-        act(R("ad"), P(6, 0, L), AF.Abs)
-        act(R("ad2"), P(6, 0, L), AF.Abs, bias=-0.5)
-        mm(P(7, 0, L), [(R("NE8"), R("th8f", m * L, m * L + L)), (R("Blk"), R("ad"))])
-        mm(P(7, L, L), [(R("Blk"), R("ad"))])
-        ts(R("st"), P(7, 0, L), 0.0 if t == 0 else R("acol"), OP.is_lt)
-        tt(R("ne"), R("st"), P(7, L, L), OP.mult)
-        tt(lanes("Wt", m), R("st"), P(6, L, L), OP.mult)
-        tt(R("u"), R("st"), P(6, 0, L), OP.mult)
-        mm(P(7, 0, L), [(R("Blk"), R("cmh")), (R("Blk"), R("ad2")), (R("Id"), R("ne"))])
-        act(R("chb"), P(7, 0, L), AF.Sign)
-        mm(P(6, 0, L), [(R("H"), R("cmh")), (R("H"), x), (R("H"), y), (R("H"), R("u"))])
-        ts(R("nx"), P(6, 0, L), C1, OP.add, C1, OP.subtract)
-        gather("a", R("Gh"), R("chb"), R("sho"))
-        gather("v" if t == 3 else "a", R("Gs"), R("nx"), R("sho"))
-        add("g", "pcp", (x, R("nx")), [R("nx")], [x], 750)
-        scan(R("cum"), R("mask5"), R("Gh"), OP.min, OP.add)
-        mm(P(7, 0, NS), [(R("N256"), R("c16")), (R("P125"), R("Gh")), (R("N512"), R("cum"))])
+            bk = bank("f")
+            mm(P(bk, 0, L), [(R("I16"), tile("Wz", j)) for j in (1, 2, 3)] + [(R("If16"), tile("m16", j)) for j in (1, 2, 3)])
+            act(R("ykb"), P(bk, 0, L))
+            add("s", "store", ("yk", "ykb", 0, L), [R("ykb")], [], 1500)
+        origin(t, [(R("Io"), R("va")), (R("Io"), tile("vb", m))] if t < 3 else [(R("Ifo"), R("O3"))])
+        e5 = opt["five"][t]
+        for a, n in opt["sp"]:
+            y, x = R("S3", 16 * a + 15, 16 * (a + n), 16), lanes("X", m, a, n)
+            st, ad, ad2, ne, u = [tile(w, 0, a, n) for w in ("st", "ad", "ad2", "ne", "u")]
+            bd, bq = bank(), bank()
+            d = P(bd, 0, n)
+            mm(d, [(R("NI"), x), (R("Id"), y)])
+            act(ad, d, AF.Abs)
+            act(ad2, d, AF.Abs, bias=-0.5)
+            mm(P(bq, 0, n), [(R("NE16"), R("th16", m * L + a, m * L + a + n, 1, 0, 2)), (R("Blk"), ad)])
+            mm(P(bq, L, n), [(R("Blk"), ad)])
+            ts(st, P(bq, 0, n), 0.0 if t == 0 else R("acol"), OP.is_lt)
+            if t < 3:
+                bn = bank()
+                mm(P(bn, 0, n), [(R("IBS"), one(n)), (R("Id"), tile("Wz", t, a, n)), (R("If"), tile("m16", t, a, n))])
+                tt(lanes("E", m, a, n), st, P(bn, 0, n), OP.mult)
+            if t == 0:
+                act(tile("Kn0", 0, a, n), P(bn, 0, n))
+            tt(ne, st, P(bq, L, n), OP.mult)
+            tt(u, st, d, OP.mult)
+            bk = bank()
+            mm(P(bk, 0, n), [(R("Blk"), ad2)], True, False)
+            mm(P(bk, 0, n), [(R("Id"), ne)], False, True)
+            if e5[0] == "a":
+                act(tile("chb", 0, a, n), P(bk, 0, n), AF.Sign, bias=-8.0)
+            else:
+                ts(tile("chb", 0, a, n), P(bk, 0, n), 8.0, OP.is_gt)
+            bk = bank()
+            mm(P(bk, 0, n), [(R("Id"), x), (R("Id"), y)], True, False)
+            mm(P(bk, 0, n), [(R("Id"), u)], False, True)
+            lin(e5[1], tile("nx", 0, a, n), P(bk, 0, n), 0.4995, C1)
+        if t == 0:
+            gcopy(R("st0"), R("st"))
+        gather(e5[2], R("Gh"), R("chb"), R("sho"))
+        gather(e5[3], R("Gs"), R("nx"), R("sho"), -C1)
+        lin(e5[4], lanes("X", m), R("nx"), 1.0, -C1)
+        scan(R("cum"), R("mask5"), R("Gh"), OP.min, OP.add, 8.0)
+        bk = bank()
+        mm(P(bk, 0, NS), [(R("P125"), R("Gh"))], True, False)
+        mm(P(bk, 0, NS), [(R("N512"), R("cum"))], False, True)
         ob = R("outb", t * NS, t * NS + NS)
-        tt(ob, R("Gs"), P(7, 0, NS), OP.min)
-        add("g", "send", (t,), [ob], [], 500)
+        tt(ob, R("Gs"), P(bk, 0, NS), OP.min)
+        add("g", "send", (t,), [ob], [R("sent", t, t + 1)], 500)
         if t < 3:
-            mm(P(7, 0, L), [(R("Id"), R("st")), (R("NE8b"), lanes("f8b", m))])
-            act(R("junk"), P(7, 0, L), AF.Abs, accum=R("cnt", 0, 1))
-            mm(P(7, 0, 2), [(R("on16"), R("cnt"))])
-            cp(R("Ai"), P(7, 0, 1))
+            bk = bank("f")
+            mm(P(bk, 0, L), [(R("Id"), R("st")), (R("NE8"), lanes("f8b", m))])
+            act(R("junk"), P(bk, 0, L), AF.Abs, accum=R("cnt", 0, 1))
+            mm(P(bk, L, 2), [(R("on16"), R("cnt"))])
+            cp(R("Ai"), P(bk, L, 1))
             ts(R("Ai2"), R("Ai"), 63, OP.bitwise_and)
             cp(R("acol"), R("Ai2"))
-            origin(t, lanes("vt", m))
         if t == 0:
-            bk = fil()
-            mm(P(bk, 0, L), [(R("If"), tile("Oacc", 0)), (R("NIf512"), tile("sq", 0))])
-            act(R("O0p"), P(bk, 0, L), AF.Identity, bias=-(OACC + OOWN))
-            ts(R("offO"), R("O0p"), OOWN, OP.add)
-            tt(R("dO"), lanes("vt", 0), R("O0p"), OP.subtract)
-            ts(R("ne0"), R("dO"), 0.0, OP.not_equal)
-            act(R("ne32"), R("ne0"), AF.Identity, scale=32.0)
-            act(R("fo"), lanes("Wt", 0), AF.Sign)
-            bk = fil()
-            mm(P(bk, 0, L), [(R("If32"), lanes("O32", 0)), (R("NI32"), lanes("Wall", 0)), (R("NIf32"), lanes("Mt", 0))])
-            mm(P(bk, L, L), [(R("Id"), lanes("Wall", 0)), (R("NI"), tile("Wn", 0))])
-            tt(R("dM"), R("ne32"), P(bk, 0, L), OP.mult)
-            tt(R("dW"), R("ne0"), P(bk, L, L), OP.mult)
-            tt(R("dWf"), R("dW"), R("fo"), OP.mult)
-    bk = big()
-    mm(P(bk, 0, L), [(R("If"), tile("Oacc", t)) for t in (1, 2)] + [(R("NIf512"), tile("sq", t)) for t in (1, 2, 3)])
-    act(R("dM"), P(bk, 0, L), AF.Identity, bias=-3 * OACC)
-    tt(R("yob"), R("dM"), tile("Oacc", 3), OP.add)
-    add("s", "store", ("yo", "yob", 0, L), [R("yob")], [], 2000)
-    act(R("yfb"), R("Wt", 0, V), AF.Sign)
+            cp(R("offO"), tile("Oi", 0))
+            tt(R("dO"), R("vt", 0, L), tile("Oi", 0), OP.subtract)
+            act(R("junk"), R("dO"), AF.Sign)
+            act(R("ne0"), R("junk"), AF.Abs)
+            bk = bank("f")
+            mm(P(bk, 0, L), [(R("If"), own(0)), (R("NIf"), R("Kn0"))])
+            tt(R("dE"), R("ne0"), P(bk, 0, L), OP.mult)
+        if t == 2:
+            tt(R("yo1"), tile("Oi", 1), tile("Oi", 2), OP.add)
+            act(R("yfb"), R("E", 0, V), AF.Sign)
+    tt(R("yob"), R("yo1"), tile("Oi", 3), OP.add)
+    add("s", "store", ("yo", "yob", 0, L), [R("yob")], [], 1500)
+    gcopy(lanes("yfb", 0), R("st"))
     for q in range(8):
-        add("s", "storef", (q,), [R("yfb")], [], 2000)
-    add("s", "store", ("yx", "X", 0, V), [R("X", 0, V)], [], 3000)
+        add("s", "storef", (q,), [R("yfb")], [], 1500)
+    add("s", "store", ("yx", "X", 0, V), [R("X", 0, V)], [], 2000)
     merge(3)
-    add("s", "store", ("yx", "X", V, W), [R("X", V, W)], [], 2500)
+    add("s", "store", ("yx", "X", V, W), [R("X", V, W)], [], 1600)
     return ops
 
 
 def meet(x, y):
     if x[3] == y[3] and (x[1] - y[1]) % x[3]:
         return False
-    return x[0] == y[0] and x[1] < y[2] and y[1] < x[2]
+    return x[1] < y[2] and y[1] < x[2] and x[4] < y[5] and y[4] < x[5]
 
 
-ASYNC = ("load", "store", "storef", "arr")
+def covers(x, y):
+    return x[1] <= y[1] and y[2] <= x[2] and x[4] <= y[4] and y[5] <= x[5] and (x[3] == 1 or (x[3] == y[3] and meet(x, y)))
 
 
-def link(ops):
+ASYNC = ("load", "load16", "store", "storef", "arr", "back")
+
+
+def link(ops, place):
     hist, turn = {}, {}
     for i, o in enumerate(ops):
         dep, order = set(), set()
         acc = [(x, False) for x in o["r"]] + [(x, True) for x in o["w"]]
         for x, wr in acc:
-            for (j, y, wy) in hist.get(x[0], []):
+            key = place.get(x[0], x[0])
+            for (j, y, wy) in hist.get(key, []):
                 if o["e"] == "t" and ops[j]["e"] == "t":
-                    order.add(j)
-                elif meet(x, y) and (wr or wy):
+                    if isps(x):
+                        order.add(j)
+                elif (wr or wy) and meet(x, y):
                     dep.add(j)
             if isps(x):
-                cur, prev = turn.get(x[0], ([], []))
+                cur, prev = turn.get(key, ([], []))
                 if cur and ops[cur[0]]["e"] != o["e"]:
                     cur, prev = [], cur
                 dep.update(prev)
-                turn[x[0]] = (cur + [i], prev)
+                turn[key] = (cur + [i], prev)
         for x, wr in acc:
-            if o["e"] == "t" and not wr:
-                if x[0] in CONST:
-                    continue
-            h = hist.setdefault(x[0], [])
+            h = hist.setdefault(place.get(x[0], x[0]), [])
             if wr:
-                h[:] = [e for e in h if not (x[1] <= e[1][1] and e[1][2] <= x[2] and (x[3] == 1 or (x[3] == e[1][3] and meet(x, e[1]))))]
+                h[:] = [e for e in h if not covers(x, e[1])]
+            elif o["e"] == "t":
+                h[:] = [e for e in h if e[2] or e[1] != x or ops[e[0]]["e"] != "t"]
             h.append((i, x, wr))
         dep.discard(i)
-        order = set(j for j in order if ops[j]["w"][0][0] == o["w"][0][0] and j != i)
+        order.discard(i)
         o["dep"], o["ord"] = dep, order - dep
-    for o in ops:
-        o["succ"] = []
-    for i, o in enumerate(ops):
-        for j in o["dep"] | o["ord"]:
-            ops[j]["succ"].append((i, j in o["dep"]))
     return ops
 
 
@@ -488,52 +618,12 @@ def cost(o, m):
     if kind == "g":
         return 60 + m[0] * m[1] * n
     if kind == "p":
-        return m[2] * n
+        return m[2] * n + m[6]
+    if kind == "f":
+        return m[7]
+    if kind == "q":
+        return n[0] + 2 * m[0] * n[1]
     return n
-
-
-def lay_out(ops, seed):
-    rs = np.random.RandomState(seed)
-    n = len(ops)
-    m = MODELS[0]
-    c = [cost(o, m) for o in ops]
-    hop = m[4]
-    wob = 1 + 0.5 * rs.rand() * (rs.rand(n) - 0.5)
-    level = [0.0] * n
-    for i in range(n - 1, -1, -1):
-        level[i] = c[i] * wob[i] + max([level[j] + (hop if d else 0) for j, d in ops[i]["succ"]] + [0.0])
-    pred = [[(j, True) for j in o["dep"]] + [(j, False) for j in o["ord"]] for o in ops]
-    succ = [o["succ"] for o in ops]
-    hold = [60 if o["kind"] in ASYNC else c[i] for i, o in enumerate(ops)]
-
-    def place(order, before, back):
-        busy = {e: [] for e in "vatgsx"}
-        t0 = [0.0] * n
-        for i in order:
-            s = max([t0[j] + c[j] + (hop if d else 0) for j, d in before[i]] + [0.0])
-            off = c[i] - hold[i] if back else 0.0
-            s += off
-            b = busy[ops[i]["e"]]
-            k = len(b)
-            while k > 0 and b[k - 1][1] > s:
-                k -= 1
-            while k < len(b) and b[k][0] < s + hold[i]:
-                s = max(s, b[k][1])
-                k += 1
-            b.insert(k, (s, s + hold[i]))
-            t0[i] = s - off
-        return t0
-
-    order = sorted(range(n), key=lambda i: (-level[i], i))
-    best = None
-    for _ in range(PASSES):
-        t0 = place(order, pred, False)
-        end = max(t0[i] + c[i] for i in range(n))
-        if best is None or end < best[0]:
-            best = (end, sorted(range(n), key=lambda i: (t0[i], i)))
-        tb = place(sorted(range(n), key=lambda i: (-(t0[i] + c[i]), -i)), succ, True)
-        order = sorted(range(n), key=lambda i: (-(tb[i] + c[i]), i))
-    return best[1]
 
 
 def units(ops):
@@ -542,18 +632,108 @@ def units(ops):
         if us and o["u"] is not None and o["u"] == ops[i - 1]["u"] and o["e"] == ops[i - 1]["e"]:
             us[-1]["ops"].append(i)
         else:
-            us.append(dict(e=o["e"], kind=o["kind"], ops=[i], succ=[]))
+            us.append(dict(e=o["e"], kind=o["kind"], ops=[i], succ=[], step=o["step"],
+                           name=o["a"][1][0] + "*" + o["a"][2][0] if o["kind"] == "mm" else o["e"] + ":" + (o["w"][0][0][:2] if o["w"] and isps(o["w"][0]) else o["w"][0][0] if o["w"] else "")))
         of[i] = len(us) - 1
     for k, u in enumerate(us):
         u["c"] = ("u", [ops[i] for i in u["ops"]])
         u["dep"] = set(of[j] for i in u["ops"] for j in ops[i]["dep"]) - {k}
         u["ord"] = set(of[j] for i in u["ops"] for j in ops[i]["ord"]) - {k} - u["dep"]
+        u["ps"] = set(x[0] for i in u["ops"] for x in ops[i]["r"] + ops[i]["w"] if isps(x))
         for j in u["dep"] | u["ord"]:
             us[j]["succ"].append((k, j in u["dep"]))
     return us
 
 
-def refine(us, seq, moves, seed):
+def backward(us, seq):
+    m = MODELS[0]
+    busy = {e: [] for e in "vatgsx"}
+    t1 = [0.0] * len(us)
+    for i in reversed(seq):
+        u, c = us[i], cost(us[i], m)
+        hold = 60 if u["kind"] in ASYNC else c
+        s = max([t1[j] + m[4] if d else t1[j] - cost(us[j], m) for j, d in u["succ"]] + [0.0]) + c - hold
+        b = busy[u["e"]]
+        k = len(b)
+        while k > 0 and b[k - 1][1] > s:
+            k -= 1
+        while k < len(b) and b[k][0] < s + hold:
+            s = max(s, b[k][1])
+            k += 1
+        b.insert(k, (s, s + hold))
+        t1[i] = s + hold
+    return t1
+
+
+def tenants(us):
+    users, below = {}, [0] * len(us)
+    for i in range(len(us) - 1, -1, -1):
+        for j, _ in us[i]["succ"]:
+            below[i] |= below[j] | 1 << j
+        for p in us[i]["ps"]:
+            users.setdefault(p, []).append(i)
+    return users, {p: set(j for i in w for j in us[i]["dep"] if j != w[-1] and not below[w[-1]] >> j & 1) for p, w in users.items()}
+
+
+def lay_out(us, opt, ahead, users, needs, given=None):
+    n, m = len(us), MODELS[0]
+    c = [cost(u, m) for u in us]
+    hop = m[4]
+    level, after = [0.0] * n, {}
+    for i in range(n - 1, -1, -1):
+        key = (us[i]["step"], us[i]["e"])
+        level[i] = c[i] + ahead.get(us[i]["name"], 0.0) + max([level[j] + (hop if d else 0) for j, d in us[i]["succ"]] + [after.get(key, 0.0)])
+        if key[0]:
+            after[key] = level[i]
+    level = given or level
+    left = {p: len(w) for p, w in users.items()}
+    slack, lean = ahead.get("slack", 300.0), ahead.get("lean", 0.0)
+    done, last = set(), 0.0
+    wait = [len(u["dep"] | u["ord"]) for u in us]
+    est = [0.0] * n
+    ready = [i for i in range(n) if not wait[i]]
+    free = {e: 0.0 for e in "vatgsx"}
+    tenant, until, place, seq = [None] * 8, [0.0] * 8, {}, []
+    while ready:
+        cand = []
+        for i in ready:
+            s, take = max(est[i], free[us[i]["e"]]), None
+            new = [p for p in us[i]["ps"] if p not in place]
+            if new:
+                ok = [b for b in range(8) if tenant[b] is None and (b in opt["fil"]) == (new[0][1] == "f")]
+                if not ok or not needs[new[0]] <= done:
+                    continue
+                take = min(ok, key=lambda b: until[b])
+                s = max(s, until[take] + hop)
+            cand.append((s, i, take))
+        if not cand:
+            return None
+        s0, i0, _ = min(cand)
+        s, i, take = max((x for x in cand if us[x[1]]["e"] == us[i0]["e"] and x[0] <= s0 + slack), key=lambda x: level[x[1]] - lean * x[0])
+        u = us[i]
+        ready.remove(i)
+        seq.append(i)
+        done.add(i)
+        end = s + c[i]
+        last = max(last, end)
+        free[u["e"]] = s + (60 if u["kind"] in ASYNC else c[i])
+        for p in u["ps"]:
+            if p not in place:
+                place[p] = take
+                tenant[take] = p
+            left[p] -= 1
+            until[place[p]] = max(until[place[p]], end)
+            if not left[p]:
+                tenant[place[p]] = None
+        for j, d in u["succ"]:
+            est[j] = max(est[j], end + hop if d else s)
+            wait[j] -= 1
+            if not wait[j]:
+                ready.append(j)
+    return seq, place, last
+
+
+def refine(us, seq, moves, seed, heat):
     rs = np.random.RandomState(seed)
     n = len(us)
     eng = ["vatgsx".index(u["e"]) for u in us]
@@ -622,17 +802,49 @@ def refine(us, seq, moves, seed):
                 continue
             new = seq[:pa] + [x for x in seq[pa:pb + 1] if x not in ts] + [x for x in seq[pa:pb + 1] if x in ts] + seq[pb + 1:]
         sc, r2 = score(new)
-        if sc <= cur + HEAT * (1 - it / moves) * rs.rand():
+        if sc <= cur + heat * (1 - it / moves) * rs.rand():
             cur, r, seq = sc, r2, new
             if sc < best[0]:
                 best = (sc, new)
-    return best[1]
+    return best
 
 
-def plan():
-    ops = link(build())
+def order(opt):
+    ops = link(build(opt), {})
     us = units(ops)
-    seq = [i for u in refine(us, lay_out(us, SEED), MOVES, SEED) for i in us[u]["ops"]]
+    users, needs = tenants(us)
+    rs = np.random.RandomState(opt["seed"])
+    names = sorted(set(u["name"] for u in us))
+    ahead = dict(opt["ahead"])
+    best = lay_out(us, opt, ahead, users, needs)
+    for _ in range(opt["tries"]):
+        new = dict(ahead)
+        for _ in range(1 + rs.randint(3)):
+            w = names[rs.randint(len(names))]
+            new[w] = new.get(w, 0.0) + 1500 * rs.randn()
+        if rs.rand() < 0.1:
+            new["slack"] = 100 + 900 * rs.rand()
+            new["lean"] = 3 * rs.rand()
+        got = lay_out(us, opt, new, users, needs)
+        if got is not None and (best is None or got[2] <= best[2]):
+            best, ahead = got, new
+    opt["found"] = ahead
+    done = None
+    for turn in range(opt["turns"]):
+        ops2 = link([dict(ops[i]) for u in best[0] for i in us[u]["ops"]], best[1])
+        us2 = units(ops2)
+        score, seq = refine(us2, list(range(len(us2))), opt["moves"], turn, opt["heat"])
+        if done is None or score < done[0]:
+            done = (score, ops2, [i for u in seq for i in us2[u]["ops"]], best[1])
+        level = [0.0] * len(us)
+        for k, u in enumerate(seq):
+            level[best[0][u]] = -float(k)
+        best = lay_out(us, opt, {"slack": 2000.0}, users, needs, level) or best
+    return done[1:]
+
+
+def plan(opt):
+    ops, seq, place = order(opt)
     pos = {i: k for k, i in enumerate(seq)}
     seen = {e: {} for e in "vatgs"}
     need = set()
@@ -664,7 +876,7 @@ def plan():
         if o["inc"]:
             count[o["e"]] += 1
             o["n"] = count[o["e"]]
-    return ops, seq, count
+    return ops, seq, place
 
 
 _PLAN = {}
@@ -675,17 +887,20 @@ def rank_program(g, core, T, topo):
     if rank is None:
         return
     if "p" not in _PLAN:
-        _PLAN["p"] = plan()
-    ops, seq, count = _PLAN["p"]
+        _PLAN["p"] = plan(OPT)
+    ops, seq, place = _PLAN["p"]
     Q = {"v": g.vector, "a": g.scalar, "t": g.tensor, "g": g, "s": g.sync}
     SEM = {e: T.sem["e_" + e] for e in "vatg"}
 
     def ap(r):
         if not isinstance(r, tuple):
             return r
+        t = T["ps%d" % place[r[0]]] if isps(r) else T[r[0]]
+        if len(shape(r[0])) == 3:
+            return t[:, r[1]:r[2], r[4]] if r[5] == r[4] + 1 else t[:, r[1]:r[2], r[4]:r[5]]
         if r[3] == 1:
-            return T[r[0]][:, r[1]:r[2]]
-        return T[r[0]][:, r[1]:r[2]:r[3]]
+            return t[:, r[1]:r[2]]
+        return t[:, r[1]:r[2]:r[3]]
 
     stores = 0
     for i in seq:
@@ -696,7 +911,7 @@ def rank_program(g, core, T, topo):
         q = Q[o["e"]]
         for j in o["wait"]:
             p = ops[j]
-            if p["kind"] == "load":
+            if p["kind"] in ("load", "load16"):
                 q.wait_ge(T.sem[p["a"][0]], 16)
             elif p["kind"] == "arr":
                 q.wait_ge(T.sem["arr%d" % p["a"][0]], N - 1)
@@ -715,7 +930,7 @@ def rank_program(g, core, T, topo):
         elif k == "ms":
             ins = q.memset(ap(a[0]), a[1])
         elif k == "scan":
-            ins = q.tensor_tensor_scan(ap(a[0]), ap(a[1]), ap(a[2]), 0.0, a[3], a[4])
+            ins = q.tensor_tensor_scan(ap(a[0]), ap(a[1]), ap(a[2]), a[5], a[3], a[4])
         elif k == "act":
             if a[5] is None:
                 ins = q.activation(ap(a[0]), ap(a[1]), a[2], bias=ap(a[3]), scale=ap(a[4]))
@@ -723,12 +938,14 @@ def rank_program(g, core, T, topo):
                 ins = q.activation(ap(a[0]), ap(a[1]), a[2], bias=ap(a[3]), scale=ap(a[4]), accum_out=ap(a[5]))
         elif k == "gat":
             src = ap(a[1]).indirect(ap(a[2]))
-            if a[3] is not None:
-                ins = q.tensor_tensor(ap(a[0]), src, ap(a[3]), OP.add)
-            elif o["e"] == "v":
+            if o["e"] == "a":
+                ins = q.activation(ap(a[0]), src, AF.Sign if a[3] == "sign" else AF.Identity, bias=0.0 if a[3] in (None, "sign") else a[3])
+            elif a[3] is None:
                 ins = q.tensor_copy(ap(a[0]), src)
+            elif a[3] == "sign":
+                ins = q.tensor_scalar(ap(a[0]), src, 0.0, None, OP.is_gt)
             else:
-                ins = q.activation(ap(a[0]), src, AF.Identity)
+                ins = q.tensor_scalar(ap(a[0]), src, a[3], None, OP.add)
         elif k == "mm":
             ins = q.matmul(ap(a[0]), ap(a[1]), ap(a[2]), a[3], a[4])
         elif k == "iota":
@@ -737,13 +954,12 @@ def rank_program(g, core, T, topo):
             else:
                 ins = q.iota(ap(a[0]), a[1], a[2], a[3], allow_small_or_imprecise_dtypes=True)
         elif k == "sel":
-            ins = q.affine_select(ap(a[0]), ap(a[1]), a[2], a[3], a[6], a[4], a[5])
-        elif k == "sel8":
-            ins = q.affine_select(ap(a[0]), T[a[1][0]][0:8, 0:128], a[2], a[3], 0.0, a[4], a[5])
+            rows = shape(a[0][0])[0]
+            ins = q.affine_select(ap(a[0]), ap(a[1]) if rows == 128 else T[a[1][0]][0:rows, 0:128], a[2], a[3], a[6], a[4], a[5])
         elif k == "load":
-            q.dma_start(T[a[1]][:, a[3]:a[4]], T[a[2]][:, a[3]:a[4]]).then_inc(T.sem[a[0]], 16)
-        elif k == "pcp":
-            ins = q.affine_select(ap(a[0]), ap(a[1]), [[0, L]], OP.is_ge, 0.0, 0, 0)
+            q.dma_start(ap(a[1]), T[a[2][0]][:, a[2][1]:a[2][2]]).then_inc(T.sem[a[0]], 16)
+        elif k == "load16":
+            q.dma_start(T.th16[8 * a[1]:8 * a[1] + 8, :], T.thb[:, 48 * a[1]:48 * a[1] + 48]).then_inc(T.sem[a[0]], 16)
         elif k == "store":
             q.dma_start(T[a[0]][:, a[2]:a[3]], T[a[1]][:, a[2]:a[3]]).then_inc(T.sem.stored, 16)
             stores += 1

import numpy as np
from concourse.bass import DstId, RemoteDMATransfer
from concourse.mybir import AluOpType as OP, ActivationFunctionType as AF

N, V, W, G, L, RO = 8, 1280, 1728, 64, 256, 4
NS = (N - 1) * G
SW = 65536.0
BS = 145 * SW
BIG = 256 * SW
C1 = 1.5 * 2.0 ** 23
C8 = 1.5 * 2.0 ** 31
HL = 64

B, F, I, U = "bfloat16", "float32", "int32", "uint16"
STEP = 215 / 2.0 ** 31
SCALED = dict(NI=-1.0, N256=-256.0, P125=12544.0, N512=-512.0, NI16=-1 / 16, I16=1 / 16, I15=15.0, IBS=BS, NBS=-BS,
              N2048=-2048.0, I2=2.0, Io=1 / 4096)
SCALED32 = dict(If=1.0, NIf=-1.0, If16=1 / 16, Ifo=1 / 4096)
_SB = dict(
    ktb=(V, I), shb=(28, I), sho=(28, U), X=(W, B), Ef=(V, F), E=(W, F),
    Eg=(4096, F), S=(4096, F), Gx=(4096, B), A3=(4096, B), S3=(4096, B),
    ones=(512, B), zero=(128, B), Id=(128, B), Blk=(128, B), Blk0=(128, B), NSel=(2048, B), Sel17=(2048, B), Dg=(2048, B),
    Pk=(1024, B), Dz=(1024, B), on16=(128, F), mask3=(1024, B), mask5=(NS, B), vt=(L, F), va=(L, B), vb=(3 * L, B),
    IdC=(128, B), IdD=(128, B), cst=(1024, B),
    pk=(16, I), pk2=(16, I), nek=(16, F), ek=(16, F), ek12=(16, F), pc=(8, F),
    ki=(2, I), kf=(4, F), colh=(1, F),
    offC=(RO * L, U), offX=(L, U), offO=(L, U), w1=(L, B), wz=(RO * L, B), hq=(L, B), hi=(RO * L, B), lo=(RO * L, B),
    b1=(L, F), ow=(RO * L, B), bh=(L, B), Wz=(RO * L, B), m16=(RO * L, F), tq=(RO * L, B), rr=(L, B), zc=(L, B), sq=(L, B),
    acc=(512, F), h0=(L, B), bi=(L, I), mi=(L, I), Qi=(L, I), Oi=(RO * L, I),
    fs=(80, I), fsb=(80, B), fsn=(80, B), ths=(48, I), thb=(96, B), st=(L, B), ad=(L, B), ad2=(L, B), u=(L, B), nx=(L, F), ne=(L, B),
    chb=(L, B), junk=(L, B), Gs=(NS, B), Gh=(NS, B), cum=(NS, B), outb=(RO * NS, B), land=(RO * NS, B), rl=(NS, B),
    cnt=(2, F), Ai=(1, I), Ai2=(1, I), acol=(1, F),
    sc=(RO * L, F), st0=(L, B), Kn0=(L, F), dO=(L, F), ne0=(L, B), dE=(L, F), Ef3=(L, F), O3=(L, F), yfb=(V, F), ykb=(L, F), yo1=(L, F), yob=(L, F),
)
for _n in SCALED:
    _SB[_n] = (128, B)
for _n in SCALED32:
    _SB[_n] = (128, F)
SCRATCH = {}
for _n, (_w, _d) in _SB.items():
    SCRATCH[_n] = ("sbuf", [128, _w], _d)
SCRATCH.update(Wr=("sbuf", [128, L, 16], B), Rl=("sbuf", [128, L, 17], B), f8b=("sbuf", [8, V], B), th16=("sbuf", [16, 768], B),
               NE8=("sbuf", [8, 128], B), NEa=("sbuf", [16, 128], B), NE16=("sbuf", [16, 128], B))
for _k in range(8):
    SCRATCH["ps%d" % _k] = ("psum", [128, 512], F)

LOADS = ["l_f", "l_k0", "l_k1", "l_k2", "l_k3", "l_th", "l_sh", "l_x", "l_f8", "l_t8", "l_t9"]
SEMAPHORES = ["e_v", "e_a", "e_t", "e_g", "stored", "sent"] + LOADS + ["arr%d" % t for t in range(RO)]

MODELS = [(0.83, 1.56, 0.42, 15.0, 130.0, 1.0, 15.0, 5000.0), (0.83, 1.15, 0.42, 10.0, 100.0, 0.7, 18.0, 6500.0),
          (0.83, 1.95, 0.42, 20.0, 160.0, 0.7, 12.0, 4000.0)]
OPT = dict(
    form=("d cc b",) * 4,
    cast=("gggg", "gggg", "gggg", "gggg"),
    small="aaa", fold=(), back=14000, gsplit=1, bits=False, rl="a", gch=1024, bh="a", wz="a", tpe=False, passes=2,
    gat=("aaaa", "aaaa", "aaaa", "aaaa"),
    gatx=("aaaa", "aaaa", "aaaa", "aaaa"),
    xp=((0, 64), (64, 128), (192, 64)),
    sp=((0, 192), (192, 64)), rp=((0, 128), (128, 128)), lov=True,
    etab="vvva",
    five=("aaaaa", "aaaaa", "aaaaa", "vavaa"), fil=(5, 6, 7), ahead={"x:land": 3000, "v:NSel": 3000, "g:Blk": 3000}, seed=1, turns=1, tries=300, moves=8000, heat=500.0, flight=4000, load=1.0,
)


def shape(name):
    return [128, 512] if name[0] == "#" else SCRATCH[name][1]


def R(name, a=0, b=None, s=1, k0=0, k1=1):
    if b is None:
        b = shape(name)[1]
    return (name, a, b, s, k0, k1)


def cnt_of(r):
    return len(range(r[1], r[2], r[3])) * (r[5] - r[4])


def isps(r):
    return r[0][0] == "#"


def two(r):
    return not isps(r) and SCRATCH[r[0]][2] in (B, U)


def build(opt):
    ops = []
    unit, step = [None], [None]

    def add(e, kind, args, reads, writes, cost):
        ops.append(dict(e=e, kind=kind, a=args, r=[x for x in reads if isinstance(x, tuple)], w=writes,
                        c=cost if isinstance(cost, tuple) else ("k", cost), u=unit[0], step=step[0]))

    def ts(out, in0, s1, op0, s2=None, op1=None):
        add("v", "ts", (out, in0, s1, s2, op0, op1), [in0, s1, s2], [out], ("v", cnt_of(out) * (0.5 if two(out) and two(in0) else 1)))

    def tt(out, a, b, op):
        add("v", "tt", (out, a, b, op), [a, b], [out], ("v", cnt_of(out) * (1 if isps(a) or isps(b) else 2)))

    def cp(out, a):
        add("v", "cp", (out, a), [a], [out], ("v", cnt_of(out) * (0.5 if two(out) and two(a) else 1)))

    def ms(out, val):
        add("v", "ms", (out, val), [], [out], ("v", cnt_of(out) * (0.5 if two(out) else 1)))

    def scan(out, d0, d1, op0, op1, first=0.0):
        add("v", "scan", (out, d0, d1, op0, op1, first), [d0, d1], [out], ("v", cnt_of(out) * (0.5 if two(out) and two(d0) and two(d1) else 1)))

    def act(out, a, func=AF.Identity, bias=0.0, scale=1.0, accum=None):
        add("a", "act", (out, a, func, bias, scale, accum), [a, bias, scale], [out] + ([accum] if accum else []), ("v", cnt_of(out)))

    def lin(e, out, a, scale, bias):
        if e == "a":
            act(out, a, AF.Identity, bias, scale)
        else:
            ts(out, a, scale, OP.mult, bias, OP.add)

    def gather(e, out, win, off, how=None):
        n = cnt_of(out)
        c = min(n, opt["gch"])
        for j in range(0, n, c):
            o, f = R(out[0], out[1] + j, out[1] + j + c), R(off[0], off[1] + j // 16, off[1] + (j + c) // 16)
            add(e, "gat", (o, win, f, how), [win, f], [o], ("g", c))

    def sel(out, src, pattern, cmp, base, mult, fill):
        add("g", "sel", (out, src, pattern, cmp, base, mult, fill), [src], [out], ("q", (170, cnt_of(out))))

    def gcopy(out, src):
        sel(out, src, [[0, cnt_of(out)]], OP.is_ge, 0, 0, 0.0)

    def iota(out, pattern, base, mult):
        add("g", "iota", (out, pattern, base, mult), [], [out], ("q", (130, cnt_of(out))))

    def mm(out, terms, first=True, last=True):
        alone = unit[0] is None
        run = 0
        for j, (l, r) in enumerate(terms):
            c = max(64, cnt_of(out)) * (1 if two(l) else 4)
            if alone and (j == 0 or run + c > 1100):
                unit[0], run = len(ops), 0
            run += c
            add("t", "mm", (out, l, r, first and j == 0, last and j == len(terms) - 1), [l, r], [out], ("p", c))
        if alone:
            unit[0] = None

    def mat(name, k=0):
        return R(name, 128 * k, 128 * k + 128)

    banks = [0]

    def bank(kind="c"):
        banks[0] += 1
        return "#%s%d" % (kind, banks[0])

    def P(bk, a, n):
        return R(bk, a, a + n)

    def one(n):
        return R("ones", 0, n)

    def dma(e, sem, dst, src, cost, reads=()):
        add(e, "load", (sem, dst, src), list(reads), [dst], cost * opt["load"])

    cuts = (0, 320, 640, 960, V)
    for j in range(4):
        dma("sa"[j % 2], "l_k%d" % j, R("ktb", cuts[j], cuts[j + 1]), ("kt", cuts[j], cuts[j + 1]), 1800 + 200 * j)
    dma("a", "l_f", R("fs"), ("f0", None, None), 1700)
    dma("s", "l_th", R("ths"), ("th", None, None), 2600)
    dma("s", "l_sh", R("shb"), ("shw", None, None), 2600)
    dma("s", "l_x", R("X"), ("x0", None, None), 3200)
    ms(R("ones"), 1.0)
    ms(R("zero"), 0.0)
    iota(R("pk"), [[-1, 16]], 16, 1)
    sel(R("Blk0"), one(128), [[-16, 8], [0, 16]], OP.is_ge, 0, 1, 0.0)
    sel(R("Blk"), R("Blk0"), [[16, 8], [0, 16]], OP.is_ge, 15, -1, 0.0)
    sel(R("Id"), one(128), [[-1, 128]], OP.is_equal, 0, 1, 0.0)
    sel(R("NE8"), R("zero"), [[1, 8], [0, 16]], OP.not_equal, 0, -1, -1.0)
    sel(R("NEa"), R("zero"), [[1, 8], [0, 16]], OP.not_equal, 0, -1, -1.0)
    sel(R("NE16"), R("NEa"), [[1, 8], [0, 16]], OP.not_equal, 8, -1, -1.0)
    sel(R("IdC"), R("Id"), [[-1, 128]], OP.not_equal, -1, 1, STEP)
    sel(R("IdD"), R("IdC"), [[-1, 128]], OP.not_equal, 127, 1, STEP)
    ms(R("cst"), 1.0)
    ms(R("cst", 0, 1024, 16), -2 * BIG)
    iota(R("vt"), [[5, L]], 0, 0)
    iota(R("va"), [[160, 8], [0, 32]], 0, 0)
    iota(R("vb"), [[1, 3], [0, 8], [5, 32]], 0, 0)
    iota(R("mask5"), [[0, N - 1], [G, G]], 8, 0)
    act(R("mask3"), R("cst"), AF.Relu, scale=256.0)
    ts(R("pk2"), R("pk"), 15, OP.bitwise_and)
    ts(R("nek"), R("pk2"), 0.0, OP.is_equal, -1.0, OP.mult)
    ts(R("ek"), R("pk2"), 0.0, OP.is_equal)
    ts(R("ek12"), R("ek"), 1 / 4096, OP.mult)
    tt(R("pc"), R("ek", 0, 16, 2), R("ek12", 1, 16, 2), OP.add)
    ki, kf = [R("ki", j, j + 1) for j in range(2)], [R("kf", j, j + 1) for j in range(4)]
    ts(ki[0], R("pk2", 0, 1), 1, OP.logical_shift_right)
    ts(kf[0], ki[0], -3.5, OP.add)
    tt(kf[1], kf[0], kf[0], OP.mult)
    ts(ki[1], R("pk2", 0, 1), 1, OP.bitwise_and)
    ts(kf[2], ki[1], 2048.0, OP.mult, -2048.0, OP.add)
    tt(kf[3], kf[1], kf[2], OP.mult)
    ts(R("colh"), kf[3], -32768.0, OP.add)
    for nm, val in SCALED.items():
        if nm in ("NI", "NI16", "I15"):
            ts(R(nm), R("Id"), val, OP.mult)
        else:
            sel(R(nm), R("zero"), [[-1, 128]], OP.not_equal, 0, 1, val)
    for nm, val in SCALED32.items():
        act(R(nm), R("Id"), scale=val)
    for k in range(16):
        ts(mat("NSel", k), R("Blk"), R("nek", k, k + 1), OP.mult)
    for k in range(2):
        sel(R("Dg", 1024 * k, 1024 * k + 1024), R("NSel", 1024 * k, 1024 * k + 1024), [[0, 8], [-1, 128]], OP.is_equal, 0, 1, 0.0)
        act(R("Sel17", 1024 * k, 1024 * k + 1024), R("NSel", 1024 * k, 1024 * k + 1024), scale=-17 / SW)
    for j in range(8):
        ts(mat("Pk", j), R("Blk"), R("pc", j, j + 1), OP.mult)
    for j in range(8):
        sel(mat("Dz", j), R("zero"), [[-1, 128]], OP.not_equal, 0, 1, 4096.0 * (j - 3.5))
    ms(R("on16"), 1 / 16)
    ms(R("Rl", 0, L, 1, 0, 1), 2 * BIG)
    ms(R("E", V, W), 0.0)
    ms(R("cnt"), 0.0)
    ts(R("fsn"), R("fs"), -BIG, OP.mult)
    cp(R("fsb"), R("fs"))
    ts(R("thb", 0, 48), R("ths"), C8, OP.add, C8, OP.subtract)
    tt(R("thb", 48, 96), R("ths"), R("thb", 0, 48), OP.subtract)
    dma("s", "l_f8", R("f8b"), ("fsb", None, None), 1600, [R("fsb")])
    add("s", "load16", ("l_t8", 0), [R("thb", 0, 48)], [R("th16", 0, 768, 1, 0, 1)], 1600)
    add("s", "load16", ("l_t9", 1), [R("thb", 48, 96)], [R("th16", 0, 768, 1, 1, 2)], 1600)
    cp(R("sho"), R("shb"))
    for j in range(4):
        a, b = cuts[j], cuts[j + 1]
        ts(R("Ef", a, b), R("ktb", a, b), 16.0, OP.mult, BS, OP.add)
        bk = bank()
        if opt["etab"][j] == "v":
            for q in range(4):
                mm(P(bk, 80 * q, 80), [(mat("NSel", a // 80 + q), R("fsn"))])
            tt(R("E", a, b), R("Ef", a, b), P(bk, 0, b - a), OP.min)
        else:
            mm(P(bk, 0, b - a), [(R("If"), R("Ef", a, b))], True, False)
            for q in range(4):
                mm(P(bk, 80 * q, 80), [(mat("NSel", a // 80 + q), R("fsn"))], False, q == 3)
            act(R("E", a, b), P(bk, 0, b - a), AF.Relu, bias=-BIG)

    def lanes(name, m, a=0, n=L):
        return R(name, m + 5 * a, 5 * (a + n), 5)

    def tile(name, t, a=0, n=L):
        return R(name, t * L + a, t * L + a + n)

    def own(t, a=0, n=L):
        return lanes("Ef", t, a, n) if t < 3 else R("Ef3", a, a + n)

    def prep(t, a=0, n=L):
        bk = bank("c" if t in (0, 3) else "f")
        y, w1, hq = P(bk, 0, n), tile("w1", 0, a, n), tile("hq", 0, a, n)
        act(w1, own(t, a, n))
        mm(y, [(R("If16"), own(t, a, n)), (R("NI16"), w1)])
        cp(tile("offC", t, a, n), y)
        lin("v" if t in (0, 3) else opt["small"][0], tile("wz", t, a, n), w1, 1.0, -BS)
        act(hq, y, bias=32768.0)
        lin(opt["small"][1], tile("hi", t, a, n), hq, 1.0, R("colh"))
        if opt["lov"]:
            ts(tile("h0", 0, a, n), hq, -32768.0, OP.add)
            tt(tile("lo", t, a, n), y, tile("h0", 0, a, n), OP.subtract)
        else:
            y = P(bank("f"), 0, n)
            mm(y, [(R("If16"), own(t, a, n)), (R("NI16"), w1), (R("NI"), hq)])
            act(tile("lo", t, a, n), y, bias=32768.0)

    def step2(t, a, HL, form):
        o, per = 16 * a, 512 // HL
        based = form in "ad"
        wz = tile("wz", t, a, HL)
        for c in range(a, a + HL, 64):
            gather(opt["gat"][t][c // 64], R("Eg", 16 * c, 16 * c + 1024), R("E"), tile("offC", t, c, 64))

        def relu(out, src):
            if based:
                ts(out, src, BS, OP.max)
            else:
                act(out, src, AF.Relu, bias=-BS)

        if form in "de":
            for k0 in range(0, 16, per):
                bk = bank()
                unit[0] = len(ops)
                for k in range(per):
                    mm(P(bk, HL * k, HL), [(mat("NSel", k0 + k), wz)])
                for k in range(per):
                    tt(R("Wr", a, a + HL, 1, k0 + k, k0 + k + 1), R("Eg", o + k0 + k, o + 16 * HL, 16), P(bk, HL * k, HL), OP.add)
                unit[0] = None
            for c in range(a, a + HL, 64):
                relu(R("Rl", c, c + 64, 1, 1, 17), R("Wr", c, c + 64, 1, 0, 16))
        else:
            n = 64 // opt["gsplit"]
            for c in range(a, a + HL, n):
                if opt["cast"][t][c // 64] == "g":
                    gcopy(R("Wr", c, c + n, 1, 0, 16), R("Eg", 16 * c, 16 * (c + n)))
                else:
                    act(R("Wr", c, c + n, 1, 0, 16), R("Eg", 16 * c, 16 * (c + n)))
            for k0 in range(0, 16, per):
                bk = bank()
                unit[0] = len(ops)
                if form == "c":
                    for k in range(per):
                        mm(P(bk, HL * k, HL), [(mat("NSel", k0 + k), wz), (R("Id"), R("Wr", a, a + HL, 1, k0 + k, k0 + k + 1))])
                    relu(P(bk, 0, 512), P(bk, 0, 512))
                    for k in range(per):
                        ek = R("Eg", o + k0 + k, o + 16 * HL, 16)
                        tt(ek, ek, P(bk, HL * k, HL), OP.subtract)
                    unit[0] = None
                    continue
                mm(P(bk, 0, 512), [(R("Id"), R("Wr", a, a + HL, 1, k0, k0 + per))], True, False)
                for k in range(per):
                    mm(R(bk, k, 512, per), [(mat("NSel", k0 + k), wz)], False, k == per - 1)
                unit[0] = None
                relu(R("Rl", a, a + HL, 1, k0 + 1, k0 + per + 1), P(bk, 0, 512))
        for c in range(o, o + 16 * HL, 1024) if form == "c" else ():
            scan(R("S", c, c + 1024), R("cst"), R("Eg", c, c + 1024), OP.add, OP.max)
        for c in range(0, HL, 32) if form != "c" else ():
            bk = bank()
            if not based:
                mm(P(bk, 0, 512), [(R("Id"), one(512))], True, False)
            mm(P(bk, 0, 512), [(R("IdD" if based else "Id"), R("Rl", a + c, a + c + 32, 1, 1, 17)),
                               (R("NI"), R("Rl", a + c, a + c + 32, 1, 0, 16))], based, True)
            scan(R("S", o + 16 * c, o + 16 * c + 512), P(bk, 0, 512), R("Eg", o + 16 * c, o + 16 * c + 512), OP.add, OP.max)

    def rival(t, pieces):
        bk, a0, n = bank(), pieces[0][0], sum(w[1] for w in pieces)
        calls = [(P(bk, 0, n), [(R("If"), own(t, a0, n)), (R("I15"), one(n))]
                  + [(mat("Dg", k), R("Wr", a0, a0 + n, 1, k, k + 1)) for k in range(16)])]
        for a, HL, form in pieces:
            more = ([(R("NI"), tile("wz", t, a, HL))] if form in "de" else []) + ([(R("NBS"), one(HL))] if form in "ad" else [])
            more += [(R("Id"), R("Rl", a, a + HL, 1, 16, 17))] if form != "c" else []
            if more:
                calls.append((P(bk, a - a0, HL), more))
        for j, (out, terms) in enumerate(calls):
            mm(out, terms, j == 0, j == len(calls) - 1)
        for a, HL, form in pieces:
            winner(t, a, HL, form, P(bk, a - a0, HL), P(bk, 128 + a - a0, HL), P(bk, 256 + a - a0, HL))

    def winner(t, a, HL, form, p1, wp, q):
        o, based = 16 * a, form in "ad"
        r15, s15 = R("Rl", a, a + HL, 1, 16, 17), R("S", o + 15, o + 16 * HL, 16)
        b1, bh = R("b1", a, a + HL), R("bh", a, a + HL)
        if opt["bits"]:
            bi, mi = R("bi", a, a + HL), R("mi", a, a + HL)
            tt(bi, s15, p1, OP.max)
            ts(mi, bi, 4, OP.logical_shift_right, 2047, OP.bitwise_and)
            cp(R("offX", a, a + HL), mi)
            tt(tile("ow", t, a, HL), s15, p1, OP.is_gt)
            cp(bh, bi)
            if based:
                tt(tile("Wz", t, a, HL), bh, r15, OP.subtract)
            elif form == "c":
                lin(opt["wz"], tile("Wz", t, a, HL), bh, 1.0, -BS)
            else:
                mm(wp, [(R("Id"), bh), (R("NI"), r15)])
                lin(opt["wz"], tile("Wz", t, a, HL), wp, 1.0, -BS)
            return
        tt(b1, s15, p1, OP.max)
        if opt["bh"] == "a":
            act(bh, b1)
        else:
            cp(bh, b1)
        tt(tile("ow", t, a, HL), s15, p1, OP.is_gt)
        mm(q, [(R("If"), b1), (R("NI"), bh)])
        if form != "c":
            mm(wp, [(R("Id"), bh), (R("NI"), r15)])
        ts(R("offX", a, a + HL), q, 1 / 16, OP.mult, -15 / 32, OP.add)
        if form != "c":
            lin(opt["wz"], tile("Wz", t, a, HL), wp, 1.0, 0.0 if based else -BS)
        else:
            lin(opt["wz"], tile("Wz", t, a, HL), bh, 1.0, -BS)
        if not opt["tpe"]:
            ts(tile("m16", t, a, HL), R("offX", a, a + HL), 16.0, OP.mult)
            tt(tile("tq", t, a, HL), tile("m16", t, a, HL), q, OP.subtract)

    def step3(t, a, n):
        o = 16 * a
        for c in range(0, n, HL):
            gather(opt["gatx"][t][(a + c) // HL], R("Gx", o + 16 * c, o + 16 * (c + HL)), R("X"), R("offX", a + c, a + c + HL))
        per = 512 // n
        for k0 in range(0, 16, per):
            bk = bank()
            unit[0] = len(ops)
            for k in range(per):
                mm(P(bk, n * k, n), [(mat("Sel17", k0 + k), tile("Wz", t, a, n))])
            for k in range(per):
                tt(R("A3", o + k0 + k, o + 16 * n, 16), R("Gx", o + k0 + k, o + 16 * n, 16), P(bk, n * k, n), OP.min)
            unit[0] = None
        for c in range(o, o + 16 * n, 1024):
            scan(R("S3", c, c + 1024), R("mask3"), R("A3", c, c + 1024), OP.min, OP.max)

    def origin(t, prev):
        bk = bank("f")
        y = P(bk, 0, L)
        if opt["tpe"]:
            terms = [(R("If"), R("b1")), (R("NI"), R("bh")), (R("NIf"), tile("m16", t)), (R("NI"), tile("ow", t))]
        else:
            terms = [(R("NI"), tile("tq", t)), (R("NI"), tile("ow", t))]
        mm(y, terms)
        act(R("rr"), y, scale=-0.5, bias=198.75)
        y = P(bk, L, L)
        mm(y, terms + [(R("I2"), R("rr"))])
        lin(opt["small"][2], R("zc"), R("rr"), 1.0, -195.5)
        act(R("sq"), R("rr"), AF.Square, bias=-195.5)
        act(tile("sc", t), y, scale=-4095.0, bias=4095.0 * 398 + 1)
        fold = t in opt["fold"]
        for j in range(0, 8, 2):
            bk = bank("f")
            for i in range(2):
                mm(P(bk, L * i, L), [(mat("Dz", j + i), R("zc")), (R("N2048"), R("sq")),
                                     (mat("Pk", j + i), tile("hi", t)), (mat("Pk", j + i), tile("lo", t))])
            if fold:
                act(R("cands", (9 * t + j) * L, (9 * t + j + 2) * L), P(bk, 0, 512))
            elif j == 0:
                act(R("acc"), P(bk, 0, 512))
            else:
                tt(R("acc"), R("acc"), P(bk, 0, 512), OP.max)
        bk = bank("f")
        mm(P(bk, 0, L), [(R("N2048"), tile("ow", t))] + prev)
        if fold:
            act(tile("cands", 9 * t + 8), P(bk, 0, L))
            add("g", "fold", (t,), [R("cands", 9 * t * L, 9 * (t + 1) * L)], [R("folded", t, t + 1)], 500)
            add("x", "back", (t,), [R("folded", t, t + 1)], [tile("pick", t)], opt["back"])
            tt(R("Qi"), tile("sc", t), tile("pick", t), OP.mult)
            ts(tile("Oi", t), R("Qi"), 4095, OP.bitwise_and)
            return
        tt(P(bk, L, L), R("acc", 0, L), P(bk, 0, L), OP.max)
        tt(P(bk, 0, L), R("acc", L, 512), P(bk, L, L), OP.max)
        tt(R("Qi"), tile("sc", t), P(bk, 0, L), OP.mult)
        ts(tile("Oi", t), R("Qi"), 4095, OP.bitwise_and)

    def merge(t):
        ld = R("land", t * NS, t * NS + NS)
        add("x", "arr", (t,), [R("sent", t, t + 1)], [ld], ("f", 0))
        if opt["rl"] == "a":
            act(R("rl"), ld, AF.Relu, bias=1.0)
        else:
            ts(R("rl"), ld, 1.0, OP.add, 0.0, OP.max)
        bk = bank()
        mm(P(bk, 0, NS), [(R("Id"), R("X", V, W))], True, False)
        mm(P(bk, 0, NS), [(R("N256"), R("rl"))], False, True)
        tt(R("X", V, W), ld, P(bk, 0, NS), OP.max)

    prep(0)
    for t in range(RO):
        m = t % 3
        if t == 3:
            for h in range(4):
                gather("av"[h % 2], R("Gx", 1024 * h, 1024 * h + 1024), R("E"), R("offO", HL * h, HL * h + HL), "sign")
            for a, n in opt["rp"]:
                bk = bank()
                fr, tk, s0 = P(bk, 0, n), P(bk, 128, n), P(bk, 256, n)
                mm(s0, [(R("Id"), tile("st0", 0, a, n))])
                mm(fr, [(R("Id"), one(n))] + [(mat("Dg", k), R("Gx", 16 * a + k, 16 * (a + n), 16)) for k in range(16)])
                tt(tk, tile("dE", 0, a, n), fr, OP.mult)
                tt(tile("Ef3", 0, a, n), tile("Kn0", 0, a, n), tk, OP.add)
                tt(lanes("E", 0, a, n), tile("Ef3", 0, a, n), s0, OP.mult)
                tt(tk, tile("dO", 0, a, n), fr, OP.mult)
                tt(tile("O3", 0, a, n), tile("Oi", 0, a, n), tk, OP.add)
                prep(3, a, n)
        step[0] = (t, 2)
        a = 0
        for word in opt["form"][t].split():
            pieces = []
            for w in word:
                pieces.append((a, 128 if w.isupper() else 64, w.lower()))
                step2(t, *pieces[-1])
                a += pieces[-1][1]
            rival(t, pieces)
        step[0] = None
        if opt["tpe"] or opt["bits"]:
            lin("v", tile("m16", t), R("offX"), 16.0, 0.0)
        if opt["bits"]:
            ts(R("mi"), R("bi"), 15, OP.bitwise_and)
            ts(tile("tq", t), R("mi"), -1.0, OP.mult)
        if t > 0:
            merge(t - 1)
        step[0] = (t, 3)
        for a, n in opt["xp"]:
            step3(t, a, n)
        step[0] = None
        if t < 2:
            prep(t + 1)
        if t == 3:
            bk = bank("f")
            mm(P(bk, 0, L), [(R("I16"), tile("Wz", j)) for j in (1, 2, 3)] + [(R("If16"), tile("m16", j)) for j in (1, 2, 3)])
            act(R("ykb"), P(bk, 0, L))
            add("s", "store", ("yk", "ykb", 0, L), [R("ykb")], [], 1500)
        origin(t, [(R("Io"), R("va")), (R("Io"), tile("vb", m))] if t < 3 else [(R("Ifo"), R("O3"))])
        e5 = opt["five"][t]
        for a, n in opt["sp"]:
            y, x = R("S3", 16 * a + 15, 16 * (a + n), 16), lanes("X", m, a, n)
            st, ad, ad2, ne, u = [tile(w, 0, a, n) for w in ("st", "ad", "ad2", "ne", "u")]
            bd, bq = bank(), bank()
            d = P(bd, 0, n)
            mm(d, [(R("NI"), x), (R("Id"), y)])
            act(ad, d, AF.Abs)
            act(ad2, d, AF.Abs, bias=-0.5)
            mm(P(bq, 0, n), [(R("NE16"), R("th16", m * L + a, m * L + a + n, 1, 0, 2)), (R("Blk"), ad)])
            mm(P(bq, L, n), [(R("Blk"), ad)])
            ts(st, P(bq, 0, n), 0.0 if t == 0 else R("acol"), OP.is_lt)
            if t < 3:
                bn = bank()
                mm(P(bn, 0, n), [(R("IBS"), one(n)), (R("Id"), tile("Wz", t, a, n)), (R("If"), tile("m16", t, a, n))])
                tt(lanes("E", m, a, n), st, P(bn, 0, n), OP.mult)
            if t == 0:
                act(tile("Kn0", 0, a, n), P(bn, 0, n))
            tt(ne, st, P(bq, L, n), OP.mult)
            tt(u, st, d, OP.mult)
            bk = bank()
            mm(P(bk, 0, n), [(R("Blk"), ad2)], True, False)
            mm(P(bk, 0, n), [(R("Id"), ne)], False, True)
            if e5[0] == "a":
                act(tile("chb", 0, a, n), P(bk, 0, n), AF.Sign, bias=-8.0)
            else:
                ts(tile("chb", 0, a, n), P(bk, 0, n), 8.0, OP.is_gt)
            bk = bank()
            mm(P(bk, 0, n), [(R("Id"), x), (R("Id"), y)], True, False)
            mm(P(bk, 0, n), [(R("Id"), u)], False, True)
            lin(e5[1], tile("nx", 0, a, n), P(bk, 0, n), 0.4995, C1)
        if t == 0:
            gcopy(R("st0"), R("st"))
        gather(e5[2], R("Gh"), R("chb"), R("sho"))
        gather(e5[3], R("Gs"), R("nx"), R("sho"), -C1)
        lin(e5[4], lanes("X", m), R("nx"), 1.0, -C1)
        scan(R("cum"), R("mask5"), R("Gh"), OP.min, OP.add, 8.0)
        bk = bank()
        mm(P(bk, 0, NS), [(R("P125"), R("Gh"))], True, False)
        mm(P(bk, 0, NS), [(R("N512"), R("cum"))], False, True)
        ob = R("outb", t * NS, t * NS + NS)
        tt(ob, R("Gs"), P(bk, 0, NS), OP.min)
        add("g", "send", (t,), [ob], [R("sent", t, t + 1)], 500)
        if t < 3:
            bk = bank("f")
            mm(P(bk, 0, L), [(R("Id"), R("st")), (R("NE8"), lanes("f8b", m))])
            act(R("junk"), P(bk, 0, L), AF.Abs, accum=R("cnt", 0, 1))
            mm(P(bk, L, 2), [(R("on16"), R("cnt"))])
            cp(R("Ai"), P(bk, L, 1))
            ts(R("Ai2"), R("Ai"), 63, OP.bitwise_and)
            cp(R("acol"), R("Ai2"))
        if t == 0:
            cp(R("offO"), tile("Oi", 0))
            tt(R("dO"), R("vt", 0, L), tile("Oi", 0), OP.subtract)
            act(R("junk"), R("dO"), AF.Sign)
            act(R("ne0"), R("junk"), AF.Abs)
            bk = bank("f")
            mm(P(bk, 0, L), [(R("If"), own(0)), (R("NIf"), R("Kn0"))])
            tt(R("dE"), R("ne0"), P(bk, 0, L), OP.mult)
        if t == 2:
            tt(R("yo1"), tile("Oi", 1), tile("Oi", 2), OP.add)
            act(R("yfb"), R("E", 0, V), AF.Sign)
    tt(R("yob"), R("yo1"), tile("Oi", 3), OP.add)
    add("s", "store", ("yo", "yob", 0, L), [R("yob")], [], 1500)
    gcopy(lanes("yfb", 0), R("st"))
    for q in range(8):
        add("s", "storef", (q,), [R("yfb")], [], 1500)
    add("s", "store", ("yx", "X", 0, V), [R("X", 0, V)], [], 2000)
    merge(3)
    add("s", "store", ("yx", "X", V, W), [R("X", V, W)], [], 1600)
    return ops


def meet(x, y):
    if x[3] == y[3] and (x[1] - y[1]) % x[3]:
        return False
    return x[1] < y[2] and y[1] < x[2] and x[4] < y[5] and y[4] < x[5]


def covers(x, y):
    return x[1] <= y[1] and y[2] <= x[2] and x[4] <= y[4] and y[5] <= x[5] and (x[3] == 1 or (x[3] == y[3] and meet(x, y)))


ASYNC = ("load", "load16", "store", "storef", "arr", "back")


def link(ops, place):
    hist, turn = {}, {}
    for i, o in enumerate(ops):
        dep, order = set(), set()
        acc = [(x, False) for x in o["r"]] + [(x, True) for x in o["w"]]
        for x, wr in acc:
            key = place.get(x[0], x[0])
            for (j, y, wy) in hist.get(key, []):
                if o["e"] == "t" and ops[j]["e"] == "t":
                    if isps(x):
                        order.add(j)
                elif (wr or wy) and meet(x, y):
                    dep.add(j)
            if isps(x):
                cur, prev = turn.get(key, ([], []))
                if cur and ops[cur[0]]["e"] != o["e"]:
                    cur, prev = [], cur
                dep.update(prev)
                turn[key] = (cur + [i], prev)
        for x, wr in acc:
            h = hist.setdefault(place.get(x[0], x[0]), [])
            if wr:
                h[:] = [e for e in h if not covers(x, e[1])]
            elif o["e"] == "t":
                h[:] = [e for e in h if e[2] or e[1] != x or ops[e[0]]["e"] != "t"]
            h.append((i, x, wr))
        dep.discard(i)
        order.discard(i)
        o["dep"], o["ord"] = dep, order - dep
    return ops


def cost(o, m):
    kind, n = o["c"]
    if kind == "u":
        return sum(cost(x, m) for x in n)
    if kind == "v":
        return m[3] + m[0] * max(64, n)
    if kind == "g":
        return 60 + m[0] * m[1] * n
    if kind == "p":
        return m[2] * n + m[6]
    if kind == "f":
        return m[7]
    if kind == "q":
        return n[0] + 2 * m[0] * n[1]
    return n


def units(ops):
    us, of = [], {}
    for i, o in enumerate(ops):
        if us and o["u"] is not None and o["u"] == ops[i - 1]["u"] and o["e"] == ops[i - 1]["e"]:
            us[-1]["ops"].append(i)
        else:
            us.append(dict(e=o["e"], kind=o["kind"], ops=[i], succ=[], step=o["step"],
                           name=o["a"][1][0] + "*" + o["a"][2][0] if o["kind"] == "mm" else o["e"] + ":" + (o["w"][0][0][:2] if o["w"] and isps(o["w"][0]) else o["w"][0][0] if o["w"] else "")))
        of[i] = len(us) - 1
    for k, u in enumerate(us):
        u["c"] = ("u", [ops[i] for i in u["ops"]])
        u["dep"] = set(of[j] for i in u["ops"] for j in ops[i]["dep"]) - {k}
        u["ord"] = set(of[j] for i in u["ops"] for j in ops[i]["ord"]) - {k} - u["dep"]
        u["ps"] = set(x[0] for i in u["ops"] for x in ops[i]["r"] + ops[i]["w"] if isps(x))
        for j in u["dep"] | u["ord"]:
            us[j]["succ"].append((k, j in u["dep"]))
    return us


def backward(us, seq):
    m = MODELS[0]
    busy = {e: [] for e in "vatgsx"}
    t1 = [0.0] * len(us)
    for i in reversed(seq):
        u, c = us[i], cost(us[i], m)
        hold = 60 if u["kind"] in ASYNC else c
        s = max([t1[j] + m[4] if d else t1[j] - cost(us[j], m) for j, d in u["succ"]] + [0.0]) + c - hold
        b = busy[u["e"]]
        k = len(b)
        while k > 0 and b[k - 1][1] > s:
            k -= 1
        while k < len(b) and b[k][0] < s + hold:
            s = max(s, b[k][1])
            k += 1
        b.insert(k, (s, s + hold))
        t1[i] = s + hold
    return t1


def tenants(us):
    users, below = {}, [0] * len(us)
    for i in range(len(us) - 1, -1, -1):
        for j, _ in us[i]["succ"]:
            below[i] |= below[j] | 1 << j
        for p in us[i]["ps"]:
            users.setdefault(p, []).append(i)
    return users, {p: set(j for i in w for j in us[i]["dep"] if j != w[-1] and not below[w[-1]] >> j & 1) for p, w in users.items()}


def lay_out(us, opt, ahead, users, needs, given=None):
    n, m = len(us), MODELS[0]
    c = [cost(u, m) for u in us]
    hop = m[4]
    level, after = [0.0] * n, {}
    for i in range(n - 1, -1, -1):
        key = (us[i]["step"], us[i]["e"])
        level[i] = c[i] + ahead.get(us[i]["name"], 0.0) + max([level[j] + (hop if d else 0) for j, d in us[i]["succ"]] + [after.get(key, 0.0)])
        if key[0]:
            after[key] = level[i]
    level = given or level
    left = {p: len(w) for p, w in users.items()}
    slack, lean = ahead.get("slack", 300.0), ahead.get("lean", 0.0)
    done, last = set(), 0.0
    wait = [len(u["dep"] | u["ord"]) for u in us]
    est = [0.0] * n
    ready = [i for i in range(n) if not wait[i]]
    free = {e: 0.0 for e in "vatgsx"}
    tenant, until, place, seq = [None] * 8, [0.0] * 8, {}, []
    while ready:
        cand = []
        for i in ready:
            s, take = max(est[i], free[us[i]["e"]]), None
            new = [p for p in us[i]["ps"] if p not in place]
            if new:
                ok = [b for b in range(8) if tenant[b] is None and (b in opt["fil"]) == (new[0][1] == "f")]
                if not ok or not needs[new[0]] <= done:
                    continue
                take = min(ok, key=lambda b: until[b])
                s = max(s, until[take] + hop)
            cand.append((s, i, take))
        if not cand:
            return None
        s0, i0, _ = min(cand)
        s, i, take = max((x for x in cand if us[x[1]]["e"] == us[i0]["e"] and x[0] <= s0 + slack), key=lambda x: level[x[1]] - lean * x[0])
        u = us[i]
        ready.remove(i)
        seq.append(i)
        done.add(i)
        end = s + c[i]
        last = max(last, end)
        free[u["e"]] = s + (60 if u["kind"] in ASYNC else c[i])
        for p in u["ps"]:
            if p not in place:
                place[p] = take
                tenant[take] = p
            left[p] -= 1
            until[place[p]] = max(until[place[p]], end)
            if not left[p]:
                tenant[place[p]] = None
        for j, d in u["succ"]:
            est[j] = max(est[j], end + hop if d else s)
            wait[j] -= 1
            if not wait[j]:
                ready.append(j)
    return seq, place, last


def refine(us, seq, moves, seed, heat):
    rs = np.random.RandomState(seed)
    n = len(us)
    eng = ["vatgsx".index(u["e"]) for u in us]
    dep = [tuple(u["dep"]) for u in us]
    pre = [u["dep"] | u["ord"] for u in us]
    cs = [[cost(u, m) for u in us] for m in MODELS]
    hs = [[60 if u["kind"] in ASYNC else c[i] for i, u in enumerate(us)] for c in cs]

    def run(sq, k):
        c, h, hop = cs[k], hs[k], MODELS[k][4]
        free, last = [0.0] * 6, [-1] * 6
        t1, why = [0.0] * n, [-1] * n
        for i in sq:
            e = eng[i]
            s, w = free[e], -2 - last[e]
            for j in dep[i]:
                if t1[j] + hop > s:
                    s, w = t1[j] + hop, j
            t1[i], why[i] = s + c[i], w
            free[e], last[e] = s + h[i], i
        return max(t1), t1, why

    def score(sq):
        r = [run(sq, k) for k in range(len(MODELS))]
        return sum(x[0] * m[5] for x, m in zip(r, MODELS)), r

    cur, r = score(seq)
    best = (cur, seq)
    for it in range(moves):
        end, t1, why = r[rs.randint(len(r))]
        i = t1.index(end)
        arcs = []
        while i != -1:
            w = why[i]
            if w <= -2:
                w = -2 - w
                arcs.append((w, i))
            i = w
        if not arcs:
            break
        a, b = arcs[rs.randint(len(arcs))]
        pa, pb = seq.index(a), seq.index(b)
        for _ in range(rs.randint(3)):
            q = pa - 1
            while q >= 0 and eng[seq[q]] != eng[b]:
                q -= 1
            if q >= 0:
                pa = q
        if rs.rand() < 0.5:
            take, want = [b], set(pre[b])
            for q in range(pb - 1, pa - 1, -1):
                if seq[q] in want:
                    take.append(seq[q])
                    want |= pre[seq[q]]
            if a in take:
                continue
            ts = set(take)
            new = seq[:pa] + take[::-1] + [x for x in seq[pa:pb] if x not in ts] + seq[pb + 1:]
        else:
            pa = seq.index(a)
            ts = {a}
            for q in range(pa + 1, pb + 1):
                if pre[seq[q]] & ts:
                    ts.add(seq[q])
            if b in ts:
                continue
            new = seq[:pa] + [x for x in seq[pa:pb + 1] if x not in ts] + [x for x in seq[pa:pb + 1] if x in ts] + seq[pb + 1:]
        sc, r2 = score(new)
        if sc <= cur + heat * (1 - it / moves) * rs.rand():
            cur, r, seq = sc, r2, new
            if sc < best[0]:
                best = (sc, new)
    return best


def order(opt):
    ops = link(build(opt), {})
    us = units(ops)
    users, needs = tenants(us)
    rs = np.random.RandomState(opt["seed"])
    names = sorted(set(u["name"] for u in us))
    ahead = dict(opt["ahead"])
    best = lay_out(us, opt, ahead, users, needs)
    for _ in range(opt["tries"]):
        new = dict(ahead)
        for _ in range(1 + rs.randint(3)):
            w = names[rs.randint(len(names))]
            new[w] = new.get(w, 0.0) + 1500 * rs.randn()
        if rs.rand() < 0.1:
            new["slack"] = 100 + 900 * rs.rand()
            new["lean"] = 3 * rs.rand()
        got = lay_out(us, opt, new, users, needs)
        if got is not None and (best is None or got[2] <= best[2]):
            best, ahead = got, new
    opt["found"] = ahead
    done = None
    for turn in range(opt["turns"]):
        ops2 = link([dict(ops[i]) for u in best[0] for i in us[u]["ops"]], best[1])
        us2 = units(ops2)
        score, seq = refine(us2, list(range(len(us2))), opt["moves"], turn, opt["heat"])
        if done is None or score < done[0]:
            done = (score, ops2, [i for u in seq for i in us2[u]["ops"]], best[1])
        level = [0.0] * len(us)
        for k, u in enumerate(seq):
            level[best[0][u]] = -float(k)
        best = lay_out(us, opt, {"slack": 2000.0}, users, needs, level) or best
    return done[1:]


def plan(opt):
    ops, seq, place = order(opt)
    pos = {i: k for k, i in enumerate(seq)}
    seen = {e: {} for e in "vatgs"}
    need = set()
    for i in seq:
        o = ops[i]
        if o["kind"] == "arr":
            o["clock"] = {}
            continue
        last = {}
        for j in o["dep"]:
            p = ops[j]
            key = p["e"] if p["kind"] not in ASYNC else ("d", j)
            if key not in last or pos[j] > pos[last[key]]:
                last[key] = j
        o["wait"] = []
        mine = seen[o["e"]]
        for key, j in sorted(last.items(), key=lambda kv: -pos[kv[1]]):
            if mine.get(key, -1) < pos[j]:
                mine[key] = pos[j]
                o["wait"].append(j)
                need.add(j)
                for k2, v in ops[j]["clock"].items():
                    mine[k2] = max(mine.get(k2, -1), v)
        o["clock"] = dict(mine)
    count = {e: 0 for e in "vatg"}
    for i in seq:
        o = ops[i]
        o["inc"] = i in need and o["kind"] not in ASYNC
        if o["inc"]:
            count[o["e"]] += 1
            o["n"] = count[o["e"]]
    return ops, seq, place


_PLAN = {}


def rank_program(g, core, T, topo):
    rank = T.rank_of(core)
    if rank is None:
        return
    if "p" not in _PLAN:
        _PLAN["p"] = plan(OPT)
    ops, seq, place = _PLAN["p"]
    Q = {"v": g.vector, "a": g.scalar, "t": g.tensor, "g": g, "s": g.sync}
    SEM = {e: T.sem["e_" + e] for e in "vatg"}

    def ap(r):
        if not isinstance(r, tuple):
            return r
        t = T["ps%d" % place[r[0]]] if isps(r) else T[r[0]]
        if len(shape(r[0])) == 3:
            return t[:, r[1]:r[2], r[4]] if r[5] == r[4] + 1 else t[:, r[1]:r[2], r[4]:r[5]]
        if r[3] == 1:
            return t[:, r[1]:r[2]]
        return t[:, r[1]:r[2]:r[3]]

    stores = 0
    for i in seq:
        o = ops[i]
        k, a = o["kind"], o["a"]
        if k == "arr":
            continue
        q = Q[o["e"]]
        for j in o["wait"]:
            p = ops[j]
            if p["kind"] in ("load", "load16"):
                q.wait_ge(T.sem[p["a"][0]], 16)
            elif p["kind"] == "arr":
                q.wait_ge(T.sem["arr%d" % p["a"][0]], N - 1)
            else:
                q.wait_ge(SEM[p["e"]], p["n"])
        ins = None
        if k == "ts":
            if a[5] is None:
                ins = q.tensor_scalar(ap(a[0]), ap(a[1]), ap(a[2]), None, a[4])
            else:
                ins = q.tensor_scalar(ap(a[0]), ap(a[1]), ap(a[2]), ap(a[3]), a[4], a[5])
        elif k == "tt":
            ins = q.tensor_tensor(ap(a[0]), ap(a[1]), ap(a[2]), a[3])
        elif k == "cp":
            ins = q.tensor_copy(ap(a[0]), ap(a[1]))
        elif k == "ms":
            ins = q.memset(ap(a[0]), a[1])
        elif k == "scan":
            ins = q.tensor_tensor_scan(ap(a[0]), ap(a[1]), ap(a[2]), a[5], a[3], a[4])
        elif k == "act":
            if a[5] is None:
                ins = q.activation(ap(a[0]), ap(a[1]), a[2], bias=ap(a[3]), scale=ap(a[4]))
            else:
                ins = q.activation(ap(a[0]), ap(a[1]), a[2], bias=ap(a[3]), scale=ap(a[4]), accum_out=ap(a[5]))
        elif k == "gat":
            src = ap(a[1]).indirect(ap(a[2]))
            if o["e"] == "a":
                ins = q.activation(ap(a[0]), src, AF.Sign if a[3] == "sign" else AF.Identity, bias=0.0 if a[3] in (None, "sign") else a[3])
            elif a[3] is None:
                ins = q.tensor_copy(ap(a[0]), src)
            elif a[3] == "sign":
                ins = q.tensor_scalar(ap(a[0]), src, 0.0, None, OP.is_gt)
            else:
                ins = q.tensor_scalar(ap(a[0]), src, a[3], None, OP.add)
        elif k == "mm":
            ins = q.matmul(ap(a[0]), ap(a[1]), ap(a[2]), a[3], a[4])
        elif k == "iota":
            if SCRATCH[a[0][0]][2] == I:
                ins = q.iota(ap(a[0]), a[1], a[2], a[3])
            else:
                ins = q.iota(ap(a[0]), a[1], a[2], a[3], allow_small_or_imprecise_dtypes=True)
        elif k == "sel":
            rows = shape(a[0][0])[0]
            ins = q.affine_select(ap(a[0]), ap(a[1]) if rows == 128 else T[a[1][0]][0:rows, 0:128], a[2], a[3], a[6], a[4], a[5])
        elif k == "load":
            q.dma_start(ap(a[1]), T[a[2][0]][:, a[2][1]:a[2][2]]).then_inc(T.sem[a[0]], 16)
        elif k == "load16":
            q.dma_start(T.th16[8 * a[1]:8 * a[1] + 8, :], T.thb[:, 48 * a[1]:48 * a[1] + 48]).then_inc(T.sem[a[0]], 16)
        elif k == "store":
            q.dma_start(T[a[0]][:, a[2]:a[3]], T[a[1]][:, a[2]:a[3]]).then_inc(T.sem.stored, 16)
            stores += 1
        elif k == "storef":
            q.dma_start(T.yf[a[0]:a[0] + 1, :], T.yfb[16 * a[0]:16 * a[0] + 1, :]).then_inc(T.sem.stored, 16)
            stores += 1
        elif k == "send":
            t = a[0]
            trs = []
            for d in range(N - 1):
                dst = T.cores[(rank - 1 - d) % N]
                rid, pid = topo.addr(dst, core)
                c = t * NS + d * G
                trs.append(RemoteDMATransfer(dst_ids=[DstId(rid=rid, pnc=pid)], dma_engine_mask=1 << topo.engines(core, dst)[d],
                                             remote_sem=T.sem["arr%d" % t], src=T.outb[:, c:c + G], dst=T.land[:, c:c + G]))
            q.remote_dma_fused(trs, local_sem=T.sem.sent)
        if o["inc"]:
            ins.then_inc(SEM[o["e"]], 1)
    g.wait_ge(T.sem.sent, RO * (N - 1))
    g.sync.wait_ge(T.sem.stored, 16 * stores)
